import numpy as np, ml_dtypes
CORES = [8,9,10,11,12,13]
N = 6
import mx_ref
BF = ml_dtypes.bfloat16
def entries(a):
    return np.ascontiguousarray(a.T).reshape(-1)
def table(e):
    return np.ascontiguousarray(np.reshape(e, (-1, 16)).T).astype(np.int32)
def cols(t, e):
    v = np.concatenate([t.reshape(128, -1, 4), np.zeros((128, 1, 4), BF)], axis=1)
    return np.ascontiguousarray(v[:, e]).reshape(128, -1)
def cut(t, i, w=512):
    return t[:, w * i:w * i + w]
def f(rng, *shape):
    return mx_ref.flush((rng.standard_normal(shape, dtype=np.float32) * np.exp2(rng.integers(-2, 3, shape[:-1] + (1,)))).astype(BF))
def wide(rng, *shape, cols=0):
    v = rng.standard_normal(shape, dtype=np.float32) * np.exp2(rng.integers(-12, 13, shape)).astype(np.float32)
    if cols: v *= np.repeat(np.exp2(rng.integers(-cols, cols + 1, shape[:-2] + (1, shape[-1] // 4))) * (rng.random(shape[:-2] + (1, shape[-1] // 4)) > 0.0625), 4, axis=-1).astype(np.float32)
    return mx_ref.flush(v.astype(BF))
T, O = 256, 2
def places(rng, dest):
    e = np.zeros((N, T), int)
    for d in range(N): e[dest == d] = d * T + rng.permutation(T)
    return np.stack([table(e[r]) for r in range(N)])
def relabel(rng):
    p = rng.permutation(N)
    if np.all((p - np.arange(N)) % N == p[0]): p[[0, 1]] = p[[1, 0]]
    return p
def setup_inputs(rng):
    e = rng.permutation(N * T).reshape(N, T)
    return {"x": f(rng, N, 128, 4 * T), "to": np.stack([table(e[r]) for r in range(N)]), "w": f(rng, N, 128, 512 * O)}
def setup_inputs_swap(rng):
    d = setup_inputs(rng); p = rng.permutation(N); dest = np.zeros((N, T), int)
    for k in range(N): dest[p[k]] = p[(k + 1) % N]
    d["to"] = places(rng, dest); return d
def setup_inputs_ones(rng):
    d = setup_inputs(rng); i = np.arange(N); n = np.ones((N, N), int); n[i, rng.permutation(N)] += T % N
    for t in range(T // N - 1): n[i, rng.permutation(N)] += N
    d["to"] = places(rng, np.stack([rng.permutation(np.repeat(i, n[r])) for r in range(N)])); return d
def setup_inputs_runs(rng):
    d = setup_inputs(rng); p = relabel(rng); s, u = rng.integers(1, N), rng.integers(0, N); g, h = rng.permutation(N), rng.permutation(N)
    n = T // N + ((g[:, None] + h) % N < T % N)
    j = (np.arange(N) + s * np.arange(N)[:, None] + u) % N
    d["to"] = places(rng, np.stack([np.repeat(p[j[r]], n[r, j[r]]) for r in range(N)])); return d
def setup_inputs_comb(rng):
    d = setup_inputs(rng); p = relabel(rng); s, u = rng.integers(1, N), rng.integers(0, N); k = rng.permutation(N); c = np.arange(T)
    d["to"] = places(rng, np.stack([p[(c + np.where(c < T - T % N, s * r + u, k[r])) % N] for r in range(N)])); return d
def setup_inputs_spread(rng):
    d = setup_inputs(rng); d["x"] = wide(rng, N, 128, 4 * T, cols=8); return d
def check_inputs(d):
    e = np.concatenate([entries(d["to"][r]) for r in range(N)])
    return [] if np.array_equal(np.sort(e), np.arange(N * T)) else ["to"]
def reference(x, to, w):
    z = np.concatenate([x[r] for r in range(N)], axis=1)
    e = np.concatenate([entries(to[r]) for r in range(N)])
    home = np.zeros(N * T, int); home[e] = np.arange(N * T)
    y = np.zeros((N, 128, O * T), np.float32)
    for d in range(N):
        v = mx_ref.quantize(cols(z, home[d * T:d * T + T]))
        for o in range(O): y[d][:, T * o:T * o + T] = mx_ref.matmul(mx_ref.quantize(np.ascontiguousarray(cut(w[d], o))), v)
    return {"y": y}

@@ -1,0 +1,368 @@
+from concourse.bass import DstId, RemoteDMATransfer
+from concourse.mybir import dt, AluOpType, ActivationFunctionType
+
+N = 6
+C1, C2 = 43, 48
+OUT = 6 * 48
+W1 = OUT + 5 * C1
+_C = "float8_e4m3fn_x4"
+_BUFS = {
+    "int32": "toh 8 p8 8 Dc 48 Dc2 64 I4 6 dest 8 P6 8 FF 56 Q6 8 U6 8",
+    "uint16": "repa 4 repd 4 pm 4 lc 2 lc2 2 tou 8 Pu 8 off1 8 l1 32 l2 18 l2o 4 l3 16",
+    "bfloat16": "xs 1024 ws 1024 cval 128 idt 256 SbT 32 Sb 32 win1 320 TR 608 Pf 128 keywin 1536 trk 1536 Xs 48 Xin 48 "
+                "cnt 64",
+    "float32": "R8 64 R16 128 Rc 128 cvr 128 F4 6 hf 1 c1 1 q6 1 eh 1 eg 1 eh2 1 pv 1 cq 3 kk4 4 k8 2 kd 7 KP 56 LR 48 "
+               "zer 32 LE 48 H2 64 Cb 264 Cd 64 B3 96 QQ 64 Z 32 X2 128 PP 128 Pq 8 e1 8 Y1 19 G 64 off 56 bf 48 OR 48 "
+               "DN 48 NG0 48 NG1 48 NG2 48 S0 48 S1 48 S2 48 B 48 b1 24 b2 8 b3 8 x1 24 x2 8 x3 8 xq 8 xw 8 uu 8 ee 8 "
+               "g2 8 Y3 64 YY 64 ys 512",
+    _C: "qx 256 qw 256 land1 512 q2 288 land2 288 q3 256",
+    "uint8": "sx 256 sw 256 lans1 512 s2 288 lans2 288 s3 256",
+}
+SCRATCH = {"ps": ("psum", [128, 2048], "float32")}
+for _d, _s in _BUFS.items():
+    _p = _s.split()
+    for _n, _w in zip(_p[0::2], _p[1::2]):
+        SCRATCH[_n] = ("sbuf", [128, int(_w)], _d)
+SEMAPHORES = ("v gi to_in x_in w_in zr f4r ac sb p_ok pf kz l1r qxr q1c q1s xsr xown cown l2r l2own q2c q2s "
+              "o2c o2s l3r qwr q3c0 q3c1 q3s0 q3s1 mm00 mm01 mm10 mm11 y00 y01 y10 y11 st rc rx rc1 rs1 rc2 rs2 ls").split()
+
+
+def _shares(src, cores, topo, flip):
+    k = cores.index(src)
+    ds = cores[k + 1:] + cores[:k]
+    ds = sorted(ds, key=lambda c: topo.die(c) == topo.die(src))
+    e = topo.engines(src, ds[0])
+    h, w = len(e) // 2, len(e) // 8
+    if flip:
+        e = e[h:] + e[:h]
+    return {c: e[:h] if i == 0 else e[h + (i - 1) * w:h + i * w] for i, c in enumerate(ds)}
+
+
+def rank_program(g, core, T, topo):
+    R = T.rank_of(core)
+    if R is None:
+        return
+    cores = list(T.cores)
+    V, A, S, E = g.vector, g.scalar, g.sync, g.tensor
+    O = AluOpType
+    add, sub, mul = O.add, O.subtract, O.mult
+    shr, band = O.arith_shift_right, O.bitwise_and
+    AF = ActivationFunctionType
+    tot, last, waited = {}, {}, {}
+    made = {}
+
+    def inc(inst, sem, n=1):
+        inst.then_inc(T.sem[sem], n)
+        tot[sem] = tot.get(sem, 0) + n
+
+    def need(sem, n=None):
+        n = tot[sem] if n is None else n
+        if waited.get(sem, 0) < n:
+            waited[sem] = n
+            V.wait_ge(T.sem[sem], n)
+
+    def w(q, sem, n):
+        q.wait_ge(T.sem[sem], n)
+
+    def ap(s):
+        s, _, off = s.partition("@")
+        f = s.split(":")
+        a = T[f[0]][:, slice(*[int(i) for i in f[1:]])] if f[1:] else T[f[0]][:]
+        return a.indirect(ap(off)) if off else a
+
+    def reads(s):
+        for n in s.replace("@", ":").split(":"):
+            if n in made:
+                need(*made[n])
+            if n in last:
+                need(*last[n])
+
+    def v(call, out, ins, *more, sem="v"):
+        for s in ins + ([out] if "@" in out else []):
+            reads(s)
+        inc(call(ap(out), *[ap(s) for s in ins], *more), sem)
+        last[out.split(":")[0].split("@")[0]] = (sem, tot[sem])
+
+    def ts(out, i, s1, s2, *ops, **k):
+        for s in (s1, s2):
+            if isinstance(s, str):
+                reads(s)
+        v(V.tensor_scalar, out, [i], *[ap(s) if isinstance(s, str) else s for s in (s1, s2)], *ops, **k)
+
+    def tt(out, i, j, op, **k):
+        v(V.tensor_tensor, out, [i, j], op, **k)
+
+    def cp(out, i, **k):
+        v(V.tensor_copy, out, [i], **k)
+
+    def scan(out, i, j, op0, op1=O.add, **k):
+        v(V.tensor_tensor_scan, out, [i, j], 0.0, op0, op1, **k)
+
+    def tr(out, i, **k):
+        v(V.transpose, out, [i], **k)
+
+    def fill(s, c=0.0, **k):
+        v(V.memset, s, [], c, **k)
+
+    def base1(r, m):
+        return 48 * m if r == m else OUT + C1 * [k for k in range(N) if k != m].index(r)
+
+    def arrivals(flip):
+        return sum(len(_shares(c, cores, topo, flip)[core]) for c in cores if c != core)
+
+    def fused(src_of, dst_of, sem, flip):
+        sh = _shares(core, cores, topo, flip)
+        t = []
+        for c in sh:
+            rid, pid, _ = topo.addr(c)
+            d = cores.index(c)
+            t.append(RemoteDMATransfer(dst_ids=[DstId(rid=rid, pnc=pid)], dma_engine_mask=sum(1 << e for e in sh[c]),
+                                       remote_sem=T.sem[sem], src=src_of(d), dst=dst_of(d)))
+            tot["ls"] = tot.get("ls", 0) + len(sh[c])
+        g.remote_dma_fused(t, local_sem=T.sem.ls)
+
+    def common(c):
+        o = [k for k in cores if k != c]
+        return [e for e in topo.engines(c, o[0]) if all(e in topo.engines(c, k) for k in o)]
+
+    for b in range(4):
+        inc((S, A)[b % 2].dma_start(T.toh[32 * b:32 * b + 32, :], T.to[:, :]), "to_in", 16)
+    inc(S.dma_start(T.xs[:, 0:512], T.x[:, 0:512]), "x_in", 16)
+    inc(A.dma_start(T.xs[:, 512:1024], T.x[:, 512:1024]), "x_in", 16)
+    inc(S.dma_start(T.ws[:], T.w[:]), "w_in", 16)
+
+    def iota(n, pat, base=0, ch=0, **k):
+        inc(g.iota(ap(n), pat, base, ch, **k), "gi")
+        made[n] = ("gi", tot["gi"])
+
+    fl = {"allow_small_or_imprecise_dtypes": True}
+    iota("p8", [[0, 8]], 0, 1)
+    iota("kk4", [[2, 4]], **fl)
+    iota("Dc", [[256, 6], [0, 8]], 256)
+    iota("kd", [[1, 7]], **fl)
+    iota("Dc2", [[0, 8], [1, 8]])
+    iota("Rc", [[0, 8], [1, 16]], **fl)
+    iota("cvr", [[16, 8], [1, 8], [128, 2]], **fl)
+    iota("k8", [[8, 2]], **fl)
+
+    def act(out, i, sem, f=AF.Copy, **k):
+        inc(A.activation(ap(out), ap(i), f, **k), sem)
+
+    def const(out, i, f=AF.Copy, **k):
+        act(out, i, "ac", f, **k)
+        made[out.split(":")[0]] = ("ac", tot["ac"])
+
+    w(A, "zr", 1)
+    for b, n in (("Cb:63:264:8", 26), ("Cb:0:8", 8), ("B3:0:32", 32), ("Cd:48:64", 16), ("G:0:8", 8), ("off:0:8", 8),
+                 ("Y3:0:32", 32), ("cnt:48:64", 16)):
+        const(b, "zer:0:%d" % n)
+    lam = [6.0 * base1(r, R) for r in range(N)] + [292.0 + R, 0.0]
+    w(A, "gi", made["kd"][1])
+    for r in range(8):
+        const("KP:%d:56:8" % r, "kd", bias=lam[r], scale=6.0 if r < 7 else -298.0)
+    for r in range(N):
+        const("LR:%d:%d" % (8 * r, 8 * r + 8), "zer:0:8", bias=lam[r] + 6.0 * R + 258)
+    w(A, "ac", made["KP"][1])
+    const("G:8:16", "KP:0:8")
+    w(A, "gi", made["Rc"][1])
+    const("R16", "Rc", AF.Sign)
+    for c in (0, 128, 256):
+        const("win1:%d:%d" % (c, min(c + 128, 320)), "Rc:0:%d" % min(128, 320 - c), scale=0.0)
+    w(A, "f4r", 1)
+    const("hf", "F4:3:4", scale=8.0)
+    const("q6", "F4:2:3", scale=-6.0)
+    for a in range(3):
+        const("cq:%d:%d" % (a, a + 1), "F4:2:3", bias=16.0 * a)
+    w(A, "ac", made["hf"][1])
+    w(A, "gi", made["cvr"][1])
+    const("cval", "cvr", AF.Identity, bias=ap("hf"))
+    w(A, "x_in", tot["x_in"])
+    act("keywin:0:1024", "xs", "kz", scale=0.0)
+    act("keywin:1024:1536", "xs:0:512", "kz", scale=0.0)
+
+    fill("zer", sem="zr")
+    ts("I4:0:1", "p8:0:1", 7, None, band)
+    ts("I4:1:2", "p8:1:2", 3, 1, shr, band)
+    ts("I4:2:3", "p8:2:3", 15, None, band)
+    ts("I4:3:4", "p8:3:4", 4, 1, shr, band)
+    ts("I4:4:5", "p8:4:5", 1, None, band)
+    ts("I4:5:6", "p8:5:6", 1, 7, shr, band)
+    cp("F4", "I4", sem="f4r")
+    ts("repa", "zer:0:4", "F4:0:1", None, add)
+    ts("repd", "kk4", "F4:1:2", None, add)
+    ts("c1", "F4:0:1", 8.0, "F4:1:2", mul, add)
+    ts("R8", "Dc2", 1.0, None, O.min)
+    ts("pm", "kk4", "c1", None, add)
+
+    need("to_in")
+    tt("LE", "toh:0:8@repa:0:3", "Dc", O.is_lt)
+    ts("dest", "toh", 8, None, shr)
+    need(*made["Cb"])
+    scan("Cb:8:56", "R8:0:48", "LE", mul)
+    tt("H2", "dest:0:8@repd", "Dc2", O.is_equal)
+    tr("B3:64:96", "Cb:15:264:8")
+    tr("B3:32:64", "Cb:7:256:8")
+    need(*made["Cd"])
+    tt("Cd:0:48", "Cb:0:48", "Cb:8:56", sub)
+    ts("eh", "F4:4:5", "F4:3:4", 10.0, O.is_equal, mul)
+    scan("QQ", "B3:32:96", "B3:0:64", add, sub)
+    tt("X2:1:128:2", "Cd:0:64@pm", "H2", mul)
+    ts("SbT", "zer", "QQ:63:64", None, add)
+    tr("Z", "QQ:32:64")
+    tr("Sb", "SbT", sem="sb")
+    tt("X2:0:128:2", "Z:0:8@repa", "H2", mul)
+    ts("eg", "F4:4:5", "F4:3:4", "F4:5:6", O.is_gt, add)
+    scan("PP", "R16", "X2", mul)
+    cp("tou", "toh")
+    ts("P6", "PP:15:128:16", 1.0 / 6, -2.5 / 6, mul, add)
+    ts("Pq", "PP:15:128:16", 48.0 / 287, None, mul)
+    cp("Pu", "PP:15:128:16", sem="p_ok")
+    tt("e1", "P6", "Pq", sub)
+    tt("pv", "eh", "eg", add)
+    ts("off1", "e1", -287.0, 16.0, mul, add)
+    ts("lc", "k8", "pv", 18.0, add, O.min)
+    cp("win1:0:320@off1:0:8", "cval")
+    need("x_in")
+    v(V.quantize_mx, "qx", [], T.sx[:], T.xs[:], sem="qxr")
+    tr("TR:0:320", "win1")
+    tr("TR:320:608", "win1:16:304")
+    ts("eh2", "F4:4:5", "F4:3:4", 32.0, O.not_equal, mul)
+    tt("Y1", "TR:0:608:32", "TR:16:608:32", add)
+    ts("lc2", "zer:0:2", "eh2", "F4:5:6", add, add)
+    cp("l1", "Y1@lc", sem="l1r")
+    need("qxr")
+    need("l1r")
+
+    def pickc(out, a, b, src, n, lst, c, e, sem):
+        inc(V.tensor_copy(T[out][:, a:b].bitcast(dt.uint32), T[src][:, 0:n].bitcast(dt.uint32).indirect(T[lst][:, c:e])), sem)
+
+    def picks(out, a, b, src, n, lst, c, e, sem):
+        inc(A.activation(T[out][:, a:b], T[src][:, 0:n].indirect(T[lst][:, c:e]), AF.Copy), sem)
+
+    pickc("land1", 0, OUT, "qx", 256, "l1", 0, 18, "q1c")
+
+    need("kz")
+    need("pf", 1)
+    cp("keywin:0:1536@tou:0:8", "Pf")
+    tr("trk", "keywin")
+    tt("Xs", "trk:0:1536:32", "trk:16:1536:32", add, sem="xsr")
+
+    need("rc", sum(len(common(c)) for c in cores if c != core))
+    need("cown", 1)
+    need(*made["G"])
+    tt("G:16:64", "cnt:0:64@pm:0:3", "KP:8:56", add)
+    scan("off:8:56", "G:15:63", "G:8:56", add, sub)
+    reads("q6")
+    v(V.tensor_tensor_scan, "bf", ["G:15:63", "G:7:55"], ap("q6"), add, sub)
+    ts("FF:0:49", "off:7:56", 1.0 / 6, R / 6 - 2.5 / 6, mul, add)
+    for a in range(3):
+        ts("NG%d" % a, "bf", 96.0 * a + 6, None, O.is_ge)
+    tt("DN", "FF:1:49", "FF:0:48", sub)
+    tt("OR", "off:%d:%d@repd:0:3" % (8 * R + 8, 8 * R + 16), "LR", add)
+    for a in range(3):
+        scan("S%d" % a, "DN", "NG%d" % a, add, mul)
+    for a in range(3):
+        ts("l2:%d:18:3" % a, "S%d:6:48:8" % a, "cq:%d:%d" % (a, a + 1), float(W1 - 1), add, O.min, sem="l2r")
+    cp("l2o:0:3", "l2:%d:%d" % (3 * R, 3 * R + 3), sem="l2own")
+    need("l2r")
+    need("q1c", 1)
+    need("rc1", arrivals(False))
+    pickc("q2", 0, 288, "land1", W1, "l2", 0, 18, "q2c")
+    need("l2own")
+    pickc("land2", 48 * R, 48 * R + 48, "land1", W1, "l2o", 0, 3, "o2c")
+    need("w_in")
+    v(V.quantize_mx, "qw", [], T.sw[:], T.ws[:], sem="qwr")
+
+    need("rx", arrivals(False))
+    need("xown", 1)
+    tt("B", "OR", "Xin", O.min)
+    tt("x1", "Xin:0:24", "Xin:24:48", add)
+    tt("b1", "B:0:24", "B:24:48", add)
+    tt("x2", "x1:0:8", "x1:8:16", add)
+    tt("b2", "b1:0:8", "b1:8:16", add)
+    tt("x3", "x2", "x1:16:24", add)
+    tt("b3", "b2", "b1:16:24", add)
+    ts("xq", "x3", 1.0 / 1024, None, mul)
+    ts("Q6", "x3", 1.0 / 6144, -3.5 / 6, mul, add)
+    tt("uu", "b3", "xq", add)
+    ts("ee", "Q6", -288.0, -91.0, mul, add)
+    ts("U6", "uu", 1.0 / 6, -3.5 / 6, mul, add)
+    ts("xw", "x3", 48.0 / 1024, None, mul)
+    tt("g2", "U6", "ee", add)
+    need(*made["Y3"])
+    tt("Y3:24:32", "g2", "xw", add)
+    tr("YY:0:32", "Y3:0:32")
+    tr("YY:32:64", "Y3:0:32")
+    tr("Y3:32:64", "YY:16:48")
+    cp("l3", "Y3:24:64@lc2:0:1", sem="l3r")
+    need("l3r")
+    need("o2c")
+    need("rc2", arrivals(False))
+    for h in range(2):
+        pickc("q3", 128 * h, 128 * h + 128, "land2", 288, "l3", 8 * h, 8 * h + 8, "q3c%d" % h)
+
+    def part(o, h):
+        return slice(256 * o + 128 * h, 256 * o + 128 * h + 128), slice(512 * (2 * o + h), 512 * (2 * o + h) + 128)
+
+    for o, h in ((0, 0), (1, 0), (0, 1)):
+        y, p = part(o, h)
+        need("mm%d%d" % (o, h), 1)
+        inc(V.tensor_copy(T.ys[:, y], T.ps[:, p]), "y%d%d" % (o, h))
+
+    w(E, "qwr", 1)
+    for h in range(2):
+        w(E, "q3c%d" % h, 1)
+        w(E, "q3s%d" % h, 1)
+        for o in ((0, 1), (1, 0))[h]:
+            inc(E.matmul_mx(T.ps[:, part(o, h)[1]], T.qw[:, 128 * o:128 * o + 128], T.sw[:, 128 * o:128 * o + 128],
+                            T.q3[:, 128 * h:128 * h + 128], T.s3[:, 128 * h:128 * h + 128], True, True), "mm%d%d" % (o, h))
+
+    w(A, "sb", 1)
+    act("cnt:%d:%d" % (8 * R, 8 * R + 8), "Sb:0:8", "cown")
+    w(A, "p_ok", 1)
+    w(A, "gi", tot["gi"] + 1)
+    act("Pf", "idt:0:256@Pu:0:8", "pf")
+    w(A, "qxr", 1)
+    w(A, "l1r", 1)
+    picks("lans1", 0, OUT, "sx", 256, "l1", 0, 18, "q1s")
+    w(A, "xsr", 1)
+    act("Xin:%d:%d" % (8 * R, 8 * R + 8), "Xs:%d:%d" % (8 * R, 8 * R + 8), "xown")
+    w(A, "l2r", 3)
+    w(A, "q1s", 1)
+    w(A, "rs1", arrivals(True))
+    picks("s2", 0, 288, "lans1", W1, "l2", 0, 18, "q2s")
+    w(A, "l2own", 1)
+    picks("lans2", 48 * R, 48 * R + 48, "lans1", W1, "l2o", 0, 3, "o2s")
+    w(A, "l3r", 1)
+    w(A, "o2s", 1)
+    w(A, "rs2", arrivals(True))
+    for h in range(2):
+        picks("s3", 128 * h, 128 * h + 128, "lans2", 288, "l3", 8 * h, 8 * h + 8, "q3s%d" % h)
+    y, p = part(1, 1)
+    w(A, "mm11", 1)
+    inc(A.activation(T.ys[:, y], T.ps[:, p], AF.Copy), "y11")
+    for q, o, h in ((S, 0, 0), (S, 1, 0), (S, 0, 1), (A, 1, 1)):
+        w(q, "y%d%d" % (o, h), 1)
+        inc(q.dma_start(T.y[:, part(o, h)[0]], T.ys[:, part(o, h)[0]]), "st", 16)
+
+    w(g, "sb", 1)
+    others = [topo.addr(c) for c in cores if c != core]
+    tot["ls"] = len(common(core))
+    g.remote_dma_fused([RemoteDMATransfer(dst_ids=[DstId(rid=a[0], pnc=a[1]) for a in others], remote_sem=T.sem.rc,
+                                          dma_engine_mask=sum(1 << e for e in common(core)), srcs=[T.Sb[:, 0:8]],
+                                          dsts=[T.cnt[:, 8 * R:8 * R + 8] for a in others])], local_sem=T.sem.ls)
+    iota("idt", [[1024, 256]], 1024, **fl)
+    w(g, "q1c", 1)
+    fused(lambda d: T.land1[:, 48 * d:48 * d + C1].bitcast(dt.uint8),
+          lambda d: T.land1[:, base1(R, d):base1(R, d) + C1].bitcast(dt.uint8), "rc1", False)
+    w(g, "q1s", 1)
+    fused(lambda d: T.lans1[:, 48 * d:48 * d + C1], lambda d: T.lans1[:, base1(R, d):base1(R, d) + C1], "rs1", True)
+    w(g, "xsr", 1)
+    fused(lambda d: T.Xs[:, 8 * d:8 * d + 8], lambda d: T.Xin[:, 8 * R:8 * R + 8], "rx", False)
+    w(g, "q2c", 1)
+    fused(lambda d: T.q2[:, 48 * d:48 * d + C2].bitcast(dt.uint8),
+          lambda d: T.land2[:, 48 * R:48 * R + C2].bitcast(dt.uint8), "rc2", False)
+    w(g, "q2s", 1)
+    fused(lambda d: T.s2[:, 48 * d:48 * d + C2], lambda d: T.lans2[:, 48 * R:48 * R + C2], "rs2", True)
+    for s in ("v", "ls", "st"):
+        w(g, s, tot[s])

@@ -5,26 +5,27 @@ N = 6
 C1, C2 = 43, 48
 OUT = 6 * 48
 W1 = OUT + 5 * C1
+W2 = 5 * OUT + C2
+FAR = 4096.0
 _C = "float8_e4m3fn_x4"
 _BUFS = {
-    "int32": "toh 8 p8 8 Dc 48 Dc2 64 I4 6 dest 8 P6 8 FF 56 Q6 8 U6 8",
-    "uint16": "repa 4 repd 4 pm 4 lc 2 lc2 2 tou 8 Pu 8 off1 8 l1 32 l2 18 l2o 4 l3 16",
-    "bfloat16": "xs 1024 ws 1024 cval 128 idt 256 SbT 32 Sb 32 win1 320 TR 608 Pf 128 keywin 1536 trk 1536 Xs 48 Xin 48 "
-                "cnt 64",
-    "float32": "R8 64 R16 128 Rc 128 cvr 128 F4 6 hf 1 c1 1 q6 1 eh 1 eg 1 eh2 1 pv 1 cq 3 kk4 4 k8 2 kd 7 KP 56 LR 48 "
-               "zer 32 LE 48 H2 64 Cb 264 Cd 64 B3 96 QQ 64 Z 32 X2 128 PP 128 Pq 8 e1 8 Y1 19 G 64 off 56 bf 48 OR 48 "
-               "DN 48 NG0 48 NG1 48 NG2 48 S0 48 S1 48 S2 48 B 48 b1 24 b2 8 b3 8 x1 24 x2 8 x3 8 xq 8 xw 8 uu 8 ee 8 "
-               "g2 8 Y3 64 YY 64 ys 512",
-    _C: "qx 256 qw 256 land1 512 q2 288 land2 288 q3 256",
-    "uint8": "sx 256 sw 256 lans1 512 s2 288 lans2 288 s3 256",
+    "int32": "toh 8 p8 8 Dc 48 r8 48 I4 6 P6 8",
+    "uint16": "repa 4 pm 4 lc 2 lc2 2 tou 8 Pu 8 off1 8 l1 32 l2 18 l3 16 px 8 pd 8",
+    "bfloat16": "xs 1024 ws 1024 cval 128 idt 256 SbT 32 Sb 32 win1 320 TR 608 Pf 128 keywin 1536 trk 1536 Xs 48 Xin 64 "
+                "cnt 80 Db 32",
+    "float32": "R8 48 cvr 128 F4 6 hf 1 c1 1 q6 1 eh 1 eg 1 eh2 1 pv 1 cq 3 k8 2 kd 8 KP 56 LC 112 M 64 CT 64 Cb 264 "
+               "B3 96 QQ 98 val 64 PP 64 Pq 8 e1 8 Y1 19 G 64 bf 48 DN 48 NG0 48 NG1 48 NG2 48 S0 48 S1 48 S2 48 "
+               "dtab 16 DR 128 XR 128 MX 128 hv 32 Y3 64 YY 64 ys 512",
+    _C: "qx 256 qw 256 land1 512 land2 %d q3 256" % W2,
+    "uint8": "sx 256 sw 256 lans1 512 lans2 %d s3 256" % W2,
 }
 SCRATCH = {"ps": ("psum", [128, 2048], "float32")}
 for _d, _s in _BUFS.items():
     _p = _s.split()
     for _n, _w in zip(_p[0::2], _p[1::2]):
         SCRATCH[_n] = ("sbuf", [128, int(_w)], _d)
-SEMAPHORES = ("v gi to_in x_in w_in zr f4r ac sb p_ok pf kz l1r qxr q1c q1s xsr xown cown l2r l2own q2c q2s "
-              "o2c o2s l3r qwr q3c0 q3c1 q3s0 q3s1 mm00 mm01 mm10 mm11 y00 y01 y10 y11 st rc rx rc1 rs1 rc2 rs2 ls").split()
+SEMAPHORES = ("v gi to_in x_in w_in zr w0 f4r ac le cd sb p_ok l1r qxr gd q1c q1s xsr du pl l2r q2c q2s "
+              "l3r qwr q3c0 q3c1 q3s0 q3s1 mm00 mm01 mm10 mm11 y00 y01 y10 y11 st rc rx rc1 rs1 rc2 rs2 ls").split()
 
 
 def _shares(src, cores, topo, flip):
@@ -32,6 +33,7 @@ def _shares(src, cores, topo, flip):
     ds = cores[k + 1:] + cores[:k]
     ds = sorted(ds, key=lambda c: topo.die(c) == topo.die(src))
     e = topo.engines(src, ds[0])
+    e = e[0::2] + e[1::2]
     h, w = len(e) // 2, len(e) // 8
     if flip:
         e = e[h:] + e[:h]
@@ -95,14 +97,11 @@ def rank_program(g, core, T, topo):
     def cp(out, i, **k):
         v(V.tensor_copy, out, [i], **k)
 
-    def scan(out, i, j, op0, op1=O.add, **k):
-        v(V.tensor_tensor_scan, out, [i, j], 0.0, op0, op1, **k)
+    def scan(out, i, j, op0, op1, first=0.0, **k):
+        v(V.tensor_tensor_scan, out, [i, j], first, op0, op1, **k)
 
     def tr(out, i, **k):
         v(V.transpose, out, [i], **k)
-
-    def fill(s, c=0.0, **k):
-        v(V.memset, s, [], c, **k)
 
     def base1(r, m):
         return 48 * m if r == m else OUT + C1 * [k for k in range(N) if k != m].index(r)
@@ -130,6 +129,9 @@ def rank_program(g, core, T, topo):
     inc(S.dma_start(T.xs[:, 0:512], T.x[:, 0:512]), "x_in", 16)
     inc(A.dma_start(T.xs[:, 512:1024], T.x[:, 512:1024]), "x_in", 16)
     inc(S.dma_start(T.ws[:], T.w[:]), "w_in", 16)
+    w(S, "qxr", 2)
+    inc(S.dma_start(T.land1[:, W1:W1 + 1].bitcast(dt.uint8), T.qx[:, 0:1].bitcast(dt.uint8)), "gd", 16)
+    inc(S.dma_start(T.lans1[:, W1:W1 + 1], T.sx[:, 0:1]), "gd", 16)
 
     def iota(n, pat, base=0, ch=0, **k):
         inc(g.iota(ap(n), pat, base, ch, **k), "gi")
@@ -137,50 +139,95 @@ def rank_program(g, core, T, topo):
 
     fl = {"allow_small_or_imprecise_dtypes": True}
     iota("p8", [[0, 8]], 0, 1)
-    iota("kk4", [[2, 4]], **fl)
     iota("Dc", [[256, 6], [0, 8]], 256)
-    iota("kd", [[1, 7]], **fl)
-    iota("Dc2", [[0, 8], [1, 8]])
-    iota("Rc", [[0, 8], [1, 16]], **fl)
+    iota("kd", [[1, 8]], **fl)
+    iota("r8", [[0, 6], [1, 8]])
     iota("cvr", [[16, 8], [1, 8], [128, 2]], **fl)
     iota("k8", [[8, 2]], **fl)
+    iota("idt", [[1, 256]], **fl)
 
-    def act(out, i, sem, f=AF.Copy, **k):
+    def act(out, i, sem="ac", f=AF.Copy, **k):
         inc(A.activation(ap(out), ap(i), f, **k), sem)
+        if sem == "ac":
+            made[out.split(":")[0]] = ("ac", tot["ac"])
 
-    def const(out, i, f=AF.Copy, **k):
-        act(out, i, "ac", f, **k)
-        made[out.split(":")[0]] = ("ac", tot["ac"])
+    def const(out, c=0.0):
+        f = [int(i) for i in out.split(":")[1:]]
+        act(out, "B3:0:%d" % len(range(*f)), bias=c)
+
+    def far(a, b):
+        act("keywin:%d:%d" % (a, b), "win1:0:%d" % (b - a), bias=-FAR)
+
+    def picks(out, a, b, src, n, lst, c, e, sem):
+        inc(A.activation(T[out][:, a:b], T[src][:, 0:n].indirect(T[lst][:, c:e]), AF.Copy), sem)
 
     w(A, "zr", 1)
-    for b, n in (("Cb:63:264:8", 26), ("Cb:0:8", 8), ("B3:0:32", 32), ("Cd:48:64", 16), ("G:0:8", 8), ("off:0:8", 8),
-                 ("Y3:0:32", 32), ("cnt:48:64", 16)):
-        const(b, "zer:0:%d" % n)
-    lam = [6.0 * base1(r, R) for r in range(N)] + [292.0 + R, 0.0]
-    w(A, "gi", made["kd"][1])
-    for r in range(8):
-        const("KP:%d:56:8" % r, "kd", bias=lam[r], scale=6.0 if r < 7 else -298.0)
-    for r in range(N):
-        const("LR:%d:%d" % (8 * r, 8 * r + 8), "zer:0:8", bias=lam[r] + 6.0 * R + 258)
-    w(A, "ac", made["KP"][1])
-    const("G:8:16", "KP:0:8")
-    w(A, "gi", made["Rc"][1])
-    const("R16", "Rc", AF.Sign)
-    for c in (0, 128, 256):
-        const("win1:%d:%d" % (c, min(c + 128, 320)), "Rc:0:%d" % min(128, 320 - c), scale=0.0)
+    for b in ("Cb:63:264:8", "Cb:0:8", "LC:0:16"):
+        const(b)
+    made.pop("LC")
+    w(A, "w0", 1)
+    far(0, 320)
+    far(320, 640)
     w(A, "f4r", 1)
-    const("hf", "F4:3:4", scale=8.0)
-    const("q6", "F4:2:3", scale=-6.0)
-    for a in range(3):
-        const("cq:%d:%d" % (a, a + 1), "F4:2:3", bias=16.0 * a)
+    act("hf", "F4:3:4", scale=8.0)
+    made["win1"] = made["keywin"]
     w(A, "ac", made["hf"][1])
+    w(A, "le", 2)
+    act("M", "LC:0:64@pm")
     w(A, "gi", made["cvr"][1])
-    const("cval", "cvr", AF.Identity, bias=ap("hf"))
-    w(A, "x_in", tot["x_in"])
-    act("keywin:0:1024", "xs", "kz", scale=0.0)
-    act("keywin:1024:1536", "xs:0:512", "kz", scale=0.0)
+    act("cval", "cvr", f=AF.Identity, bias=ap("hf"))
+    w(A, "cd", 1)
+    act("CT", "LC:48:112@pm")
+    act("keywin:640:1280", "keywin:0:640")
+    act("keywin:1280:1536", "keywin:0:256")
+    w(A, "p_ok", 1)
+    w(A, "gi", made["idt"][1])
+    act("Pf", "idt:0:256@Pu:0:8")
+    w(A, "sb", 1)
+    act("cnt:%d:%d" % (8 * R + 16, 8 * R + 24), "Sb:0:8")
+    const("cnt:64:80")
+    const("cnt:15:16", 255.0)
+    lam = [6.0 * base1(r, R) for r in range(N)] + [291.0 + R, 0.0]
+    for r in range(8):
+        act("KP:%d:56:8" % r, "kd:0:7", bias=lam[r], scale=-6.0 if r < 7 else 298.0)
+    w(A, "qxr", 2)
+    w(A, "l1r", 1)
+    picks("lans1", 0, OUT, "sx", 256, "l1", 0, 18, "q1s")
+    w(A, "ac", made["KP"][1])
+    const("G:0:8")
+    act("G:8:14", "KP:0:6", bias=255.0)
+    act("G:14:16", "KP:6:8")
+    act("q6", "F4:2:3", scale=-6.0)
+    for a in range(3):
+        act("cq:%d:%d" % (a, a + 1), "F4:2:3", bias=16.0 * a + 2.5 / 6)
+    lift = 6 * 130 - 2.5
+    for b, c in (("Xin:48:64", -FAR), ("Db:3:32:4", 0.0), ("hv:0:32:4", 0.0), ("hv:1:32:4", -6.0), ("hv:2:32:4", float(OUT)),
+                 ("hv:3:32:4", 1.0), ("dtab:0:9:8", -4 * FAR), ("dtab:1:7", 6.0), ("dtab:7:8", lift + 6),
+                 ("dtab:15:16", lift + 255 + 30 + 12)):
+        const(b, c)
+    w(A, "xsr", 1)
+    act("Xin:%d:%d" % (8 * R, 8 * R + 8), "Xs:%d:%d" % (8 * R, 8 * R + 8))
+    w(A, "l2r", 3)
+    w(A, "q1s", 1)
+    w(A, "gd", 32)
+    w(A, "rs1", arrivals(True))
+    picks("lans2", 240 * R, 240 * R + OUT, "lans1", W1 + 1, "l2", 0, 18, "q2s")
+    w(A, "du", 1)
+    w(A, "pl", 2)
+    w(A, "ac", tot["ac"])
+    act("DR", "dtab:0:16@pd", bias=-6.0)
+    w(A, "rx", arrivals(False))
+    act("XR", "Xin:0:64@px")
+    w(A, "l3r", 1)
+    w(A, "q2s", 1)
+    w(A, "rs2", arrivals(True))
+    for h in range(2):
+        picks("s3", 128 * h, 128 * h + 128, "lans2", W2, "l3", 8 * h, 8 * h + 8, "q3s%d" % h)
+    for n in ("Xin", "dtab"):
+        made.pop(n)
 
-    fill("zer", sem="zr")
+    v(V.memset, "B3:0:32", [], 0.0, sem="zr")
+    v(V.memset, "win1", [], 0.0, sem="w0")
     ts("I4:0:1", "p8:0:1", 7, None, band)
     ts("I4:1:2", "p8:1:2", 3, 1, shr, band)
     ts("I4:2:3", "p8:2:3", 15, None, band)
@@ -188,118 +235,95 @@ def rank_program(g, core, T, topo):
     ts("I4:4:5", "p8:4:5", 1, None, band)
     ts("I4:5:6", "p8:5:6", 1, 7, shr, band)
     cp("F4", "I4", sem="f4r")
-    ts("repa", "zer:0:4", "F4:0:1", None, add)
-    ts("repd", "kk4", "F4:1:2", None, add)
+    ts("repa", "B3:0:4", "F4:0:1", None, add)
     ts("c1", "F4:0:1", 8.0, "F4:1:2", mul, add)
-    ts("R8", "Dc2", 1.0, None, O.min)
-    ts("pm", "kk4", "c1", None, add)
+    ts("R8", "r8", 1.0, None, O.min)
+    ts("pm", "kd:0:4", 2.0, "c1", mul, add, sem="le")
 
     need("to_in")
-    tt("LE", "toh:0:8@repa:0:3", "Dc", O.is_lt)
-    ts("dest", "toh", 8, None, shr)
-    need(*made["Cb"])
-    scan("Cb:8:56", "R8:0:48", "LE", mul)
-    tt("H2", "dest:0:8@repd", "Dc2", O.is_equal)
+    tt("LC:16:64", "toh:0:8@repa:0:3", "Dc", O.is_lt, sem="le")
+    ts("pd", "B3:0:8", "F4:2:3", None, add, sem="pl")
+    need(*made.pop("Cb"))
+    scan("Cb:8:56", "R8", "LC:16:64", mul, add)
+    ts("eh", "F4:4:5", "F4:3:4", 10.0, O.is_equal, mul)
     tr("B3:64:96", "Cb:15:264:8")
     tr("B3:32:64", "Cb:7:256:8")
-    need(*made["Cd"])
-    tt("Cd:0:48", "Cb:0:48", "Cb:8:56", sub)
-    ts("eh", "F4:4:5", "F4:3:4", 10.0, O.is_equal, mul)
-    scan("QQ", "B3:32:96", "B3:0:64", add, sub)
-    tt("X2:1:128:2", "Cd:0:64@pm", "H2", mul)
-    ts("SbT", "zer", "QQ:63:64", None, add)
-    tr("Z", "QQ:32:64")
-    tr("Sb", "SbT", sem="sb")
-    tt("X2:0:128:2", "Z:0:8@repa", "H2", mul)
+    tt("LC:64:112", "Cb:8:56", "Cb:0:48", sub, sem="cd")
+    scan("QQ:2:66", "B3:0:64", "B3:32:96", add, sub, 255.0)
     ts("eg", "F4:4:5", "F4:3:4", "F4:5:6", O.is_gt, add)
-    scan("PP", "R16", "X2", mul)
+    reads("QQ")
+    zero, qq = T.B3[:, 0:32], T.QQ[:, 65:66]
+    tr("QQ:66:98", "QQ:34:66")
+    inc(V.tensor_scalar(T.SbT[:], zero, qq, None, add), "v")
+    last["SbT"] = ("v", tot["v"])
+    tt("val", "QQ:64:72@repa", "CT", add)
+    tr("Sb", "SbT", sem="sb")
+    scan("PP", "val", "M", O.max, mul)
     cp("tou", "toh")
-    ts("P6", "PP:15:128:16", 1.0 / 6, -2.5 / 6, mul, add)
-    ts("Pq", "PP:15:128:16", 48.0 / 287, None, mul)
-    cp("Pu", "PP:15:128:16", sem="p_ok")
+    ts("P6", "PP:7:64:8", 1.0 / 6, -2.5 / 6, mul, add)
+    ts("Pq", "PP:7:64:8", 48.0 / 287, None, mul)
+    cp("Pu", "PP:7:64:8", sem="p_ok")
     tt("e1", "P6", "Pq", sub)
     tt("pv", "eh", "eg", add)
     ts("off1", "e1", -287.0, 16.0, mul, add)
-    ts("lc", "k8", "pv", 18.0, add, O.min)
-    cp("win1:0:320@off1:0:8", "cval")
     need("x_in")
-    v(V.quantize_mx, "qx", [], T.sx[:], T.xs[:], sem="qxr")
+    inc(V.quantize_mx(T.qx[:, 0:128], T.sx[:, 0:128], T.xs[:, 0:512]), "qxr")
+    cp("win1:0:320@off1:0:8", "cval")
+    inc(V.quantize_mx(T.qx[:, 128:256], T.sx[:, 128:256], T.xs[:, 512:1024]), "qxr")
     tr("TR:0:320", "win1")
     tr("TR:320:608", "win1:16:304")
-    ts("eh2", "F4:4:5", "F4:3:4", 32.0, O.not_equal, mul)
+    ts("lc", "k8", "pv", 18.0, add, O.min)
     tt("Y1", "TR:0:608:32", "TR:16:608:32", add)
-    ts("lc2", "zer:0:2", "eh2", "F4:5:6", add, add)
+    ts("eh2", "eh", -3.2, 34.0, mul, add)
     cp("l1", "Y1@lc", sem="l1r")
+    ts("px", "kd", "c1", "F4:1:2", add, sub, sem="pl")
     need("qxr")
     need("l1r")
 
     def pickc(out, a, b, src, n, lst, c, e, sem):
         inc(V.tensor_copy(T[out][:, a:b].bitcast(dt.uint32), T[src][:, 0:n].bitcast(dt.uint32).indirect(T[lst][:, c:e])), sem)
 
-    def picks(out, a, b, src, n, lst, c, e, sem):
-        inc(A.activation(T[out][:, a:b], T[src][:, 0:n].indirect(T[lst][:, c:e]), AF.Copy), sem)
-
     pickc("land1", 0, OUT, "qx", 256, "l1", 0, 18, "q1c")
 
-    need("kz")
-    need("pf", 1)
     cp("keywin:0:1536@tou:0:8", "Pf")
+    ts("lc2:0:1", "F4:5:6", 4.0, "eh2", mul, add)
     tr("trk", "keywin")
-    tt("Xs", "trk:0:1536:32", "trk:16:1536:32", add, sem="xsr")
-
     need("rc", sum(len(common(c)) for c in cores if c != core))
-    need("cown", 1)
-    need(*made["G"])
-    tt("G:16:64", "cnt:0:64@pm:0:3", "KP:8:56", add)
-    scan("off:8:56", "G:15:63", "G:8:56", add, sub)
+    need(*made.pop("G"))
+    tt("G:16:64", "cnt:16:80@pm:0:3", "KP:8:56", add)
+    tt("Xs", "trk:0:1536:32", "trk:16:1536:32", O.max, sem="xsr")
     reads("q6")
-    v(V.tensor_tensor_scan, "bf", ["G:15:63", "G:7:55"], ap("q6"), add, sub)
-    ts("FF:0:49", "off:7:56", 1.0 / 6, R / 6 - 2.5 / 6, mul, add)
+    scan("bf", "G:7:55", "G:15:63", add, sub, ap("q6"))
+    tt("DN", "G:7:55", "G:16:64", sub)
     for a in range(3):
         ts("NG%d" % a, "bf", 96.0 * a + 6, None, O.is_ge)
-    tt("DN", "FF:1:49", "FF:0:48", sub)
-    tt("OR", "off:%d:%d@repd:0:3" % (8 * R + 8, 8 * R + 16), "LR", add)
     for a in range(3):
         scan("S%d" % a, "DN", "NG%d" % a, add, mul)
     for a in range(3):
-        ts("l2:%d:18:3" % a, "S%d:6:48:8" % a, "cq:%d:%d" % (a, a + 1), float(W1 - 1), add, O.min, sem="l2r")
-    cp("l2o:0:3", "l2:%d:%d" % (3 * R, 3 * R + 3), sem="l2own")
+        ts("l2:%d:18:3" % a, "S%d:6:48:8" % a, 1.0 / 6, "cq:%d:%d" % (a, a + 1), mul, add, sem="l2r")
+    tt("dtab:9:15", "cnt:%d:72:8" % (24 + R), "cnt:%d:%d:8" % (15 + R, 56 + R), sub, sem="du")
     need("l2r")
     need("q1c", 1)
+    need("gd", 32)
     need("rc1", arrivals(False))
-    pickc("q2", 0, 288, "land1", W1, "l2", 0, 18, "q2c")
-    need("l2own")
-    pickc("land2", 48 * R, 48 * R + 48, "land1", W1, "l2o", 0, 3, "o2c")
+    pickc("land2", 240 * R, 240 * R + OUT, "land1", W1 + 1, "l2", 0, 18, "q2c")
     need("w_in")
     v(V.quantize_mx, "qw", [], T.sw[:], T.ws[:], sem="qwr")
 
-    need("rx", arrivals(False))
-    need("xown", 1)
-    tt("B", "OR", "Xin", O.min)
-    tt("x1", "Xin:0:24", "Xin:24:48", add)
-    tt("b1", "B:0:24", "B:24:48", add)
-    tt("x2", "x1:0:8", "x1:8:16", add)
-    tt("b2", "b1:0:8", "b1:8:16", add)
-    tt("x3", "x2", "x1:16:24", add)
-    tt("b3", "b2", "b1:16:24", add)
-    ts("xq", "x3", 1.0 / 1024, None, mul)
-    ts("Q6", "x3", 1.0 / 6144, -3.5 / 6, mul, add)
-    tt("uu", "b3", "xq", add)
-    ts("ee", "Q6", -288.0, -91.0, mul, add)
-    ts("U6", "uu", 1.0 / 6, -3.5 / 6, mul, add)
-    ts("xw", "x3", 48.0 / 1024, None, mul)
-    tt("g2", "U6", "ee", add)
-    need(*made["Y3"])
-    tt("Y3:24:32", "g2", "xw", add)
+    scan("MX", "DR", "XR", add, O.max)
+    need(*made.pop("Db"))
+    ts("Db:0:32:2", "MX:7:128:8", 1.0 / 6, None, mul)
+    cp("Db:1:32:4", "MX:6:128:16")
+    scan("Y3:0:32", "hv", "Db", mul, add)
     tr("YY:0:32", "Y3:0:32")
     tr("YY:32:64", "Y3:0:32")
     tr("Y3:32:64", "YY:16:48")
-    cp("l3", "Y3:24:64@lc2:0:1", sem="l3r")
+    ts("l3", "Y3:0:64@lc2:0:1", OUT * 780.0 - 130, None, add, sem="l3r")
     need("l3r")
-    need("o2c")
+    need("q2c")
     need("rc2", arrivals(False))
     for h in range(2):
-        pickc("q3", 128 * h, 128 * h + 128, "land2", 288, "l3", 8 * h, 8 * h + 8, "q3c%d" % h)
+        pickc("q3", 128 * h, 128 * h + 128, "land2", W2, "l3", 8 * h, 8 * h + 8, "q3c%d" % h)
 
     def part(o, h):
         return slice(256 * o + 128 * h, 256 * o + 128 * h + 128), slice(512 * (2 * o + h), 512 * (2 * o + h) + 128)
@@ -316,28 +340,6 @@ def rank_program(g, core, T, topo):
         for o in ((0, 1), (1, 0))[h]:
             inc(E.matmul_mx(T.ps[:, part(o, h)[1]], T.qw[:, 128 * o:128 * o + 128], T.sw[:, 128 * o:128 * o + 128],
                             T.q3[:, 128 * h:128 * h + 128], T.s3[:, 128 * h:128 * h + 128], True, True), "mm%d%d" % (o, h))
-
-    w(A, "sb", 1)
-    act("cnt:%d:%d" % (8 * R, 8 * R + 8), "Sb:0:8", "cown")
-    w(A, "p_ok", 1)
-    w(A, "gi", tot["gi"] + 1)
-    act("Pf", "idt:0:256@Pu:0:8", "pf")
-    w(A, "qxr", 1)
-    w(A, "l1r", 1)
-    picks("lans1", 0, OUT, "sx", 256, "l1", 0, 18, "q1s")
-    w(A, "xsr", 1)
-    act("Xin:%d:%d" % (8 * R, 8 * R + 8), "Xs:%d:%d" % (8 * R, 8 * R + 8), "xown")
-    w(A, "l2r", 3)
-    w(A, "q1s", 1)
-    w(A, "rs1", arrivals(True))
-    picks("s2", 0, 288, "lans1", W1, "l2", 0, 18, "q2s")
-    w(A, "l2own", 1)
-    picks("lans2", 48 * R, 48 * R + 48, "lans1", W1, "l2o", 0, 3, "o2s")
-    w(A, "l3r", 1)
-    w(A, "o2s", 1)
-    w(A, "rs2", arrivals(True))
-    for h in range(2):
-        picks("s3", 128 * h, 128 * h + 128, "lans2", 288, "l3", 8 * h, 8 * h + 8, "q3s%d" % h)
     y, p = part(1, 1)
     w(A, "mm11", 1)
     inc(A.activation(T.ys[:, y], T.ps[:, p], AF.Copy), "y11")
@@ -350,8 +352,7 @@ def rank_program(g, core, T, topo):
     tot["ls"] = len(common(core))
     g.remote_dma_fused([RemoteDMATransfer(dst_ids=[DstId(rid=a[0], pnc=a[1]) for a in others], remote_sem=T.sem.rc,
                                           dma_engine_mask=sum(1 << e for e in common(core)), srcs=[T.Sb[:, 0:8]],
-                                          dsts=[T.cnt[:, 8 * R:8 * R + 8] for a in others])], local_sem=T.sem.ls)
-    iota("idt", [[1024, 256]], 1024, **fl)
+                                          dsts=[T.cnt[:, 8 * R + 16:8 * R + 24] for a in others])], local_sem=T.sem.ls)
     w(g, "q1c", 1)
     fused(lambda d: T.land1[:, 48 * d:48 * d + C1].bitcast(dt.uint8),
           lambda d: T.land1[:, base1(R, d):base1(R, d) + C1].bitcast(dt.uint8), "rc1", False)
@@ -359,10 +360,11 @@ def rank_program(g, core, T, topo):
     fused(lambda d: T.lans1[:, 48 * d:48 * d + C1], lambda d: T.lans1[:, base1(R, d):base1(R, d) + C1], "rs1", True)
     w(g, "xsr", 1)
     fused(lambda d: T.Xs[:, 8 * d:8 * d + 8], lambda d: T.Xin[:, 8 * R:8 * R + 8], "rx", False)
+    mine = 240 * R
     w(g, "q2c", 1)
-    fused(lambda d: T.q2[:, 48 * d:48 * d + C2].bitcast(dt.uint8),
-          lambda d: T.land2[:, 48 * R:48 * R + C2].bitcast(dt.uint8), "rc2", False)
+    fused(lambda d: T.land2[:, mine + 48 * d:mine + 48 * d + C2].bitcast(dt.uint8),
+          lambda d: T.land2[:, OUT * R:OUT * R + C2].bitcast(dt.uint8), "rc2", False)
     w(g, "q2s", 1)
-    fused(lambda d: T.s2[:, 48 * d:48 * d + C2], lambda d: T.lans2[:, 48 * R:48 * R + C2], "rs2", True)
-    for s in ("v", "ls", "st"):
+    fused(lambda d: T.lans2[:, mine + 48 * d:mine + 48 * d + C2], lambda d: T.lans2[:, OUT * R:OUT * R + C2], "rs2", True)
+    for s in ("v", "ls", "st", "gi", "ac"):
         w(g, s, tot[s])

@@ -3,19 +3,21 @@ from concourse.mybir import dt, AluOpType, ActivationFunctionType
 
 N = 6
 C1, C2 = 43, 48
-OUT = 6 * 48
-W1 = OUT + 5 * C1
-W2 = 5 * OUT + C2
-FAR = 4096.0
+HEAD = 272
+W1 = HEAD + 5 * C1
+OUT = 6 * C2
+W2 = 6 * OUT
+FAR = 4096
+LIFT = 130
 _C = "float8_e4m3fn_x4"
 _BUFS = {
-    "int32": "toh 8 p8 8 Dc 48 r8 48 I4 6 P6 8",
-    "uint16": "repa 4 pm 4 lc 2 lc2 2 tou 8 Pu 8 off1 8 l1 32 l2 18 l3 16 px 8 pd 8",
-    "bfloat16": "xs 1024 ws 1024 cval 128 idt 256 SbT 32 Sb 32 win1 320 TR 608 Pf 128 keywin 1536 trk 1536 Xs 48 Xin 64 "
-                "cnt 80 Db 32",
-    "float32": "R8 48 cvr 128 F4 6 hf 1 c1 1 q6 1 eh 1 eg 1 eh2 1 pv 1 cq 3 k8 2 kd 8 KP 56 LC 112 M 64 CT 64 Cb 264 "
-               "B3 96 QQ 98 val 64 PP 64 Pq 8 e1 8 Y1 19 G 64 bf 48 DN 48 NG0 48 NG1 48 NG2 48 S0 48 S1 48 S2 48 "
-               "dtab 16 DR 128 XR 128 MX 128 hv 32 Y3 64 YY 64 ys 512",
+    "int32": "toh 8 p8 8 Dc 48 I4 6 P6 8",
+    "uint16": "repa 4 pm 4 lc 2 lc2 2 tou 8 Pu 8 off1 8 l1 32 l2 36 l3 16 px 8 pd 8 pg 4",
+    "bfloat16": "xs 1024 ws 1024 cval 128 idt 256 SbT 32 Sb 32 win1 304 TR 576 Pf 128 keywin 1536 trk 1536 "
+                "Xin 112 cnt 80 Db 32",
+    "float32": "cvr 128 F4 6 hf 1 c1 1 eh 1 eg 1 eh2 1 pv 1 cq 3 k8 2 kd 8 KP 64 LC 64 M 64 CT 64 Cb 272 "
+               "B3 97 QQ 100 val 64 PP 64 Pq 8 e1 8 Y1 18 G 64 bf 48 DN 48 NG0 48 NG1 48 NG2 48 S0 48 S1 48 S2 48 "
+               "dtab 16 DR 128 XR 128 MX 128 hv 32 Y3 96 t2 1 t3 1 ys 512",
     _C: "qx 256 qw 256 land1 512 land2 %d q3 256" % W2,
     "uint8": "sx 256 sw 256 lans1 512 lans2 %d s3 256" % W2,
 }
@@ -24,20 +26,38 @@ for _d, _s in _BUFS.items():
     _p = _s.split()
     for _n, _w in zip(_p[0::2], _p[1::2]):
         SCRATCH[_n] = ("sbuf", [128, int(_w)], _d)
-SEMAPHORES = ("v gi to_in x_in w_in zr w0 f4r ac le cd sb p_ok l1r qxr gd q1c q1s xsr du pl l2r q2c q2s "
+SEMAPHORES = ("v gi to_in x_in w_in zr w0 f4r ac le cd sb p_ok l1r qxr gd q1c q1s xsr du pl l2r l2d q2c q2s "
               "l3r qwr q3c0 q3c1 q3s0 q3s1 mm00 mm01 mm10 mm11 y00 y01 y10 y11 st rc rx rc1 rs1 rc2 rs2 ls").split()
 
 
 def _shares(src, cores, topo, flip):
     k = cores.index(src)
-    ds = cores[k + 1:] + cores[:k]
-    ds = sorted(ds, key=lambda c: topo.die(c) == topo.die(src))
+    ds = sorted(cores[k + 1:] + cores[:k], key=lambda c: topo.die(c) == topo.die(src))
     e = topo.engines(src, ds[0])
     e = e[0::2] + e[1::2]
     h, w = len(e) // 2, len(e) // 8
     if flip:
         e = e[h:] + e[:h]
-    return {c: e[:h] if i == 0 else e[h + (i - 1) * w:h + i * w] for i, c in enumerate(ds)}
+    return {c: e[h + (i - 1) * w:h + i * w] if i else e[:h] for i, c in enumerate(ds)}
+
+
+def _even(src, cores, topo):
+    k = cores.index(src)
+    ds = sorted(cores[k + 1:] + cores[:k], key=lambda c: (c == cores[k ^ 1], topo.die(c) == topo.die(src)))
+    e = topo.engines(src, ds[0])
+    e = e[0::2] + e[1::2]
+    w = len(e) // 4
+    return {c: e[i * w:(i + 1) * w] for i, c in enumerate(ds[:4])}, {ds[4]: e}
+
+
+def _halves(src, cores, topo):
+    h = cores.index(src) // 3
+    far, near = cores[3 - 3 * h:6 - 3 * h], [c for c in cores[3 * h:3 * h + 3] if c != src]
+    far = sorted(far, key=lambda c: topo.die(c) == topo.die(src))
+    e = topo.engines(src, far[0])
+    e = e[0::2] + e[1::2]
+    q = len(e) // 4
+    return {far[0]: e[:2 * q], far[1]: e[2 * q:3 * q], far[2]: e[3 * q:]}, {near[0]: e[:2 * q], near[1]: e[2 * q:]}
 
 
 def rank_program(g, core, T, topo):
@@ -104,20 +124,24 @@ def rank_program(g, core, T, topo):
         v(V.transpose, out, [i], **k)
 
     def base1(r, m):
-        return 48 * m if r == m else OUT + C1 * [k for k in range(N) if k != m].index(r)
+        return C1 * m if r == m else HEAD + C1 * [k for k in range(N) if k != m].index(r)
 
-    def arrivals(flip):
-        return sum(len(_shares(c, cores, topo, flip)[core]) for c in cores if c != core)
+    arrivals = sum(len(_shares(c, cores, topo, False)[core]) for c in cores if c != core)
 
-    def fused(src_of, dst_of, sem, flip):
-        sh = _shares(core, cores, topo, flip)
+    arrive2 = sum(len(sh.get(core, [])) for c in cores if c != core for sh in _even(c, cores, topo))
+
+    def exchange(buf, at, to, n, sem, flip, sh=None):
+        sh = sh or _shares(core, cores, topo, flip)
         t = []
         for c in sh:
             rid, pid, _ = topo.addr(c)
             d = cores.index(c)
+            src, dst = T[buf][:, at(d):at(d) + n], T[buf][:, to(d):to(d) + n]
+            if SCRATCH[buf][2] == _C:
+                src, dst = src.bitcast(dt.uint8), dst.bitcast(dt.uint8)
             t.append(RemoteDMATransfer(dst_ids=[DstId(rid=rid, pnc=pid)], dma_engine_mask=sum(1 << e for e in sh[c]),
-                                       remote_sem=T.sem[sem], src=src_of(d), dst=dst_of(d)))
-            tot["ls"] = tot.get("ls", 0) + len(sh[c])
+                                       remote_sem=T.sem[sem], src=src, dst=dst))
+            tot["ls"] += len(sh[c])
         g.remote_dma_fused(t, local_sem=T.sem.ls)
 
     def common(c):
@@ -128,23 +152,54 @@ def rank_program(g, core, T, topo):
         inc((S, A)[b % 2].dma_start(T.toh[32 * b:32 * b + 32, :], T.to[:, :]), "to_in", 16)
     inc(S.dma_start(T.xs[:, 0:512], T.x[:, 0:512]), "x_in", 16)
     inc(A.dma_start(T.xs[:, 512:1024], T.x[:, 512:1024]), "x_in", 16)
+    w(S, "x_in", 32)
     inc(S.dma_start(T.ws[:], T.w[:]), "w_in", 16)
     w(S, "qxr", 2)
     inc(S.dma_start(T.land1[:, W1:W1 + 1].bitcast(dt.uint8), T.qx[:, 0:1].bitcast(dt.uint8)), "gd", 16)
     inc(S.dma_start(T.lans1[:, W1:W1 + 1], T.sx[:, 0:1]), "gd", 16)
 
-    def iota(n, pat, base=0, ch=0, **k):
+    def iota(n, pat, base=0, ch=0):
+        b = n.split(":")[0]
+        k = {} if SCRATCH[b][2] == "int32" else {"allow_small_or_imprecise_dtypes": True}
         inc(g.iota(ap(n), pat, base, ch, **k), "gi")
-        made[n] = ("gi", tot["gi"])
+        made[b] = ("gi", tot["gi"])
 
-    fl = {"allow_small_or_imprecise_dtypes": True}
     iota("p8", [[0, 8]], 0, 1)
     iota("Dc", [[256, 6], [0, 8]], 256)
-    iota("kd", [[1, 8]], **fl)
-    iota("r8", [[0, 6], [1, 8]])
-    iota("cvr", [[16, 8], [1, 8], [128, 2]], **fl)
-    iota("k8", [[8, 2]], **fl)
-    iota("idt", [[1, 256]], **fl)
+    iota("kd", [[1, 8]])
+    iota("cvr", [[16, 8], [1, 8], [128, 2]])
+    iota("k8", [[8, 2]])
+    iota("idt", [[1, 256]])
+    lam = [-298] + [6 * base1(r, R) for r in range(N)] + [33.5 + R]
+    for k in range(3):
+        iota("KP:%d:64:8" % k, [[-6 if k else 298, 8]], lam[k])
+    ramps = made.pop("KP")
+    w(g, "sb", 1)
+    others = [topo.addr(c) for c in cores if c != core]
+    tot["ls"] = len(common(core))
+    g.remote_dma_fused([RemoteDMATransfer(dst_ids=[DstId(rid=a[0], pnc=a[1]) for a in others], remote_sem=T.sem.rc,
+                                          dma_engine_mask=sum(1 << e for e in common(core)), srcs=[T.Sb[:, 0:8]],
+                                          dsts=[T.cnt[:, 8 * R + 16:8 * R + 24] for a in others])], local_sem=T.sem.ls)
+    sizes = sum(len(common(c)) for c in cores if c != core)
+    mine = OUT * R
+    iota("Xin:48:64", [[0, 16]], -FAR)
+    pad = made.pop("Xin")
+    iota("hv:0:32:2", [[0, 8], [OUT, 2]])
+    iota("hv:1:32:2", [[0, 8], [7, 2]], -6)
+    iota("Db:3:32:4", [[0, 8]])
+    for buf, ready, sem in (("lans1", "q1s", "rs1"), ("land1", "q1c", "rc1")):
+        w(g, ready, 1)
+        for sh in _even(core, cores, topo):
+            exchange(buf, lambda d: C1 * d, lambda d: base1(R, d), C1, sem, False, sh)
+    w(g, "xsr", 1)
+    for sh in _even(core, cores, topo):
+        exchange("Xin", lambda d: 64 + 8 * d, lambda d: 8 * R, 8, "rx", False, sh)
+    for buf, ready, sem in (("land2", "q2c", "rc2"), ("lans2", "q2s", "rs2")):
+        w(g, ready, 1)
+        for sh in _even(core, cores, topo):
+            exchange(buf, lambda d: mine + C2 * (d - R), lambda d: mine, C2, sem, False, sh)
+    runs1 = ((0, 17),)
+    runs2 = ((0, 18),)
 
     def act(out, i, sem="ac", f=AF.Copy, **k):
         inc(A.activation(ap(out), ap(i), f, **k), sem)
@@ -155,78 +210,75 @@ def rank_program(g, core, T, topo):
         f = [int(i) for i in out.split(":")[1:]]
         act(out, "B3:0:%d" % len(range(*f)), bias=c)
 
-    def far(a, b):
-        act("keywin:%d:%d" % (a, b), "win1:0:%d" % (b - a), bias=-FAR)
-
     def picks(out, a, b, src, n, lst, c, e, sem):
         inc(A.activation(T[out][:, a:b], T[src][:, 0:n].indirect(T[lst][:, c:e]), AF.Copy), sem)
 
     w(A, "zr", 1)
-    for b in ("Cb:63:264:8", "Cb:0:8", "LC:0:16"):
+    for b in ("LC:0:16", "Cb:71:272:8", "Cb:0:16"):
         const(b)
     made.pop("LC")
     w(A, "w0", 1)
-    far(0, 320)
-    far(320, 640)
+    act("keywin:0:304", "win1", bias=-float(FAR))
+    made["win1"] = made["keywin"]
     w(A, "f4r", 1)
     act("hf", "F4:3:4", scale=8.0)
-    made["win1"] = made["keywin"]
     w(A, "ac", made["hf"][1])
+    act("keywin:304:576", "keywin:0:272")
     w(A, "le", 2)
     act("M", "LC:0:64@pm")
+    w(A, "cd", 1)
+    act("CT", "Cb:0:64@pm")
+    w(A, "ac", made["M"][1])
+    const("M:7:64:8", 43.0 / 257)
     w(A, "gi", made["cvr"][1])
     act("cval", "cvr", f=AF.Identity, bias=ap("hf"))
-    w(A, "cd", 1)
-    act("CT", "LC:48:112@pm")
-    act("keywin:640:1280", "keywin:0:640")
-    act("keywin:1280:1536", "keywin:0:256")
+    w(A, "ac", made["keywin"][1])
+    act("keywin:576:1152", "keywin:0:576")
+    act("keywin:1152:1536", "keywin:0:384")
     w(A, "p_ok", 1)
     w(A, "gi", made["idt"][1])
     act("Pf", "idt:0:256@Pu:0:8")
     w(A, "sb", 1)
     act("cnt:%d:%d" % (8 * R + 16, 8 * R + 24), "Sb:0:8")
-    const("cnt:64:80")
-    const("cnt:15:16", 255.0)
-    lam = [6.0 * base1(r, R) for r in range(N)] + [291.0 + R, 0.0]
-    for r in range(8):
-        act("KP:%d:56:8" % r, "kd:0:7", bias=lam[r], scale=-6.0 if r < 7 else 298.0)
+    const("cnt:0:16", 256.0)
+    const("cnt:64:80", 256.0)
+    for k in range(3, 8):
+        act("KP:%d:64:8" % k, "kd", bias=float(lam[k]), scale=-6.0)
     w(A, "qxr", 2)
     w(A, "l1r", 1)
-    picks("lans1", 0, OUT, "sx", 256, "l1", 0, 18, "q1s")
-    w(A, "ac", made["KP"][1])
-    const("G:0:8")
-    act("G:8:14", "KP:0:6", bias=255.0)
-    act("G:14:16", "KP:6:8")
-    act("q6", "F4:2:3", scale=-6.0)
-    for a in range(3):
-        act("cq:%d:%d" % (a, a + 1), "F4:2:3", bias=16.0 * a + 2.5 / 6)
-    lift = 6 * 130 - 2.5
-    for b, c in (("Xin:48:64", -FAR), ("Db:3:32:4", 0.0), ("hv:0:32:4", 0.0), ("hv:1:32:4", -6.0), ("hv:2:32:4", float(OUT)),
-                 ("hv:3:32:4", 1.0), ("dtab:0:9:8", -4 * FAR), ("dtab:1:7", 6.0), ("dtab:7:8", lift + 6),
-                 ("dtab:15:16", lift + 255 + 30 + 12)):
-        const(b, c)
+    for a, b in runs1:
+        picks("lans1", 16 * a, 16 * b, "sx", 256, "l1", a, b, "q1s")
+    const("dtab:0:9:8", -4.0 * FAR)
+    const("dtab:1:8", 6.0)
+    const("dtab:15:16", 42.0)
+    w(A, "ac", made["cnt"][1])
+    w(A, "rc", sizes)
+    for t in range(1, 7):
+        act("dtab:%d:%d" % (8 + t, 9 + t), "cnt:%d:%d" % (7 + 8 * t + R, 8 + 8 * t + R), f=AF.Identity, scale=-1.0,
+            bias=ap("cnt:%d:%d" % (16 + 8 * t + R, 17 + 8 * t + R)))
+    w(A, "pl", 1)
+    w(A, "ac", made["dtab"][1])
+    act("DR", "dtab:0:16@pd", bias=-6.0)
     w(A, "xsr", 1)
-    act("Xin:%d:%d" % (8 * R, 8 * R + 8), "Xs:%d:%d" % (8 * R, 8 * R + 8))
+    act("Xin:%d:%d" % (8 * R, 8 * R + 8), "Xin:%d:%d" % (64 + 8 * R, 72 + 8 * R))
     w(A, "l2r", 3)
     w(A, "q1s", 1)
     w(A, "gd", 32)
-    w(A, "rs1", arrivals(True))
-    picks("lans2", 240 * R, 240 * R + OUT, "lans1", W1 + 1, "l2", 0, 18, "q2s")
-    w(A, "du", 1)
-    w(A, "pl", 2)
+    w(A, "rs1", arrive2)
+    for a, b in runs2:
+        picks("lans2", mine + 16 * (a - 3 * R), mine + 16 * (b - 3 * R), "lans1", W1 + 1, "l2", a, b, "q2s")
     w(A, "ac", tot["ac"])
-    act("DR", "dtab:0:16@pd", bias=-6.0)
-    w(A, "rx", arrivals(False))
-    act("XR", "Xin:0:64@px")
+    w(A, *pad)
+    w(A, "pl", 2)
+    w(A, "rx", arrive2)
+    act("XR:64:128", "Xin:0:64@px:4:8")
     w(A, "l3r", 1)
     w(A, "q2s", 1)
-    w(A, "rs2", arrivals(True))
+    w(A, "rs2", arrive2)
     for h in range(2):
         picks("s3", 128 * h, 128 * h + 128, "lans2", W2, "l3", 8 * h, 8 * h + 8, "q3s%d" % h)
-    for n in ("Xin", "dtab"):
-        made.pop(n)
 
-    v(V.memset, "B3:0:32", [], 0.0, sem="zr")
+    v(V.memset, "B3:0:65", [], 0.0, sem="zr")
     v(V.memset, "win1", [], 0.0, sem="w0")
     ts("I4:0:1", "p8:0:1", 7, None, band)
     ts("I4:1:2", "p8:1:2", 3, 1, shr, band)
@@ -237,93 +289,99 @@ def rank_program(g, core, T, topo):
     cp("F4", "I4", sem="f4r")
     ts("repa", "B3:0:4", "F4:0:1", None, add)
     ts("c1", "F4:0:1", 8.0, "F4:1:2", mul, add)
-    ts("R8", "r8", 1.0, None, O.min)
+    ts("pd", "B3:0:8", "F4:2:3", None, add, sem="pl")
     ts("pm", "kd:0:4", 2.0, "c1", mul, add, sem="le")
 
     need("to_in")
     tt("LC:16:64", "toh:0:8@repa:0:3", "Dc", O.is_lt, sem="le")
-    ts("pd", "B3:0:8", "F4:2:3", None, add, sem="pl")
+    cp("tou", "toh")
     need(*made.pop("Cb"))
-    scan("Cb:8:56", "R8", "LC:16:64", mul, add)
-    ts("eh", "F4:4:5", "F4:3:4", 10.0, O.is_equal, mul)
-    tr("B3:64:96", "Cb:15:264:8")
-    tr("B3:32:64", "Cb:7:256:8")
-    tt("LC:64:112", "Cb:8:56", "Cb:0:48", sub, sem="cd")
-    scan("QQ:2:66", "B3:0:64", "B3:32:96", add, sub, 255.0)
+    scan("Cb:16:64", "LC:16:64", "LC:8:56", add, sub, sem="cd")
+    ts("eh", "F4:4:5", "F4:3:4", 9.0, O.is_equal, mul)
+    tr("B3:65:97", "Cb:23:272:8")
+    tr("B3:32:64", "Cb:15:264:8")
     ts("eg", "F4:4:5", "F4:3:4", "F4:5:6", O.is_gt, add)
-    reads("QQ")
-    zero, qq = T.B3[:, 0:32], T.QQ[:, 65:66]
-    tr("QQ:66:98", "QQ:34:66")
-    inc(V.tensor_scalar(T.SbT[:], zero, qq, None, add), "v")
+    scan("QQ:1:66", "B3:0:65", "B3:32:97", add, sub, 256.0)
+    tt("pv", "eh", "eg", add)
+    tr("QQ:66:98", "QQ:33:65")
+    inc(V.tensor_scalar(T.SbT[:], T.B3[:, 0:32], T.QQ[:, 65:66], None, add), "v")
     last["SbT"] = ("v", tot["v"])
-    tt("val", "QQ:64:72@repa", "CT", add)
+    tt("val", "QQ:64:72@repa", "CT", sub)
     tr("Sb", "SbT", sem="sb")
     scan("PP", "val", "M", O.max, mul)
-    cp("tou", "toh")
-    ts("P6", "PP:7:64:8", 1.0 / 6, -2.5 / 6, mul, add)
-    ts("Pq", "PP:7:64:8", 48.0 / 287, None, mul)
-    cp("Pu", "PP:7:64:8", sem="p_ok")
-    tt("e1", "P6", "Pq", sub)
-    tt("pv", "eh", "eg", add)
-    ts("off1", "e1", -287.0, 16.0, mul, add)
+    ts("lc", "k8", "pv", 17.0, add, O.min)
+    ts("P6", "PP:7:64:8", 257.0 / 258, -2.5 / 6, mul, add)
+    ts("Pu", "PP:7:64:8", 257.0 / 43, None, mul, sem="p_ok")
+    tt("e1", "P6", "PP:7:64:8", sub)
+    ts("eh2", "eh", -1.0, 9.0, mul, add)
+    ts("off1", "e1", -257.0, 16.0, mul, add)
+    ts("pg", "pm", 7.0, None, add)
+    cp("win1:0:304@off1:0:8", "cval")
     need("x_in")
     inc(V.quantize_mx(T.qx[:, 0:128], T.sx[:, 0:128], T.xs[:, 0:512]), "qxr")
-    cp("win1:0:320@off1:0:8", "cval")
+    tr("TR:0:288", "win1:0:288")
+    tr("TR:288:576", "win1:16:304")
     inc(V.quantize_mx(T.qx[:, 128:256], T.sx[:, 128:256], T.xs[:, 512:1024]), "qxr")
-    tr("TR:0:320", "win1")
-    tr("TR:320:608", "win1:16:304")
-    ts("lc", "k8", "pv", 18.0, add, O.min)
-    tt("Y1", "TR:0:608:32", "TR:16:608:32", add)
-    ts("eh2", "eh", -3.2, 34.0, mul, add)
+    tt("Y1", "TR:0:576:32", "TR:16:576:32", add)
+    ts("cq", "kd:0:3", 16.0, "F4:2:3", mul, add)
     cp("l1", "Y1@lc", sem="l1r")
-    ts("px", "kd", "c1", "F4:1:2", add, sub, sem="pl")
+    cp("keywin:0:1536@tou:0:8", "Pf")
     need("qxr")
     need("l1r")
 
     def pickc(out, a, b, src, n, lst, c, e, sem):
         inc(V.tensor_copy(T[out][:, a:b].bitcast(dt.uint32), T[src][:, 0:n].bitcast(dt.uint32).indirect(T[lst][:, c:e])), sem)
 
-    pickc("land1", 0, OUT, "qx", 256, "l1", 0, 18, "q1c")
+    for a, b in runs1:
+        pickc("land1", 16 * a, 16 * b, "qx", 256, "l1", a, b, "q1c")
 
-    cp("keywin:0:1536@tou:0:8", "Pf")
-    ts("lc2:0:1", "F4:5:6", 4.0, "eh2", mul, add)
     tr("trk", "keywin")
-    need("rc", sum(len(common(c)) for c in cores if c != core))
-    need(*made.pop("G"))
-    tt("G:16:64", "cnt:16:80@pm:0:3", "KP:8:56", add)
-    tt("Xs", "trk:0:1536:32", "trk:16:1536:32", O.max, sem="xsr")
-    reads("q6")
-    scan("bf", "G:7:55", "G:15:63", add, sub, ap("q6"))
-    tt("DN", "G:7:55", "G:16:64", sub)
+    need(*ramps)
+    need("rc", sizes)
+    tt("G", "cnt@pg", "KP", add)
+    own = made.pop("Xin")
+    tt("Xin:64:112", "trk:0:1536:32", "trk:16:1536:32", O.max, sem="xsr")
+    scan("bf", "G:0:48", "G:8:56", add, sub, 298 - 5.5)
+    tt("DN", "G:0:48", "G:9:57", sub)
     for a in range(3):
-        ts("NG%d" % a, "bf", 96.0 * a + 6, None, O.is_ge)
+        ts("NG%d" % a, "bf", 1.0 / 6, "cq:%d:%d" % (a, a + 1), mul, O.is_gt)
     for a in range(3):
         scan("S%d" % a, "DN", "NG%d" % a, add, mul)
     for a in range(3):
         ts("l2:%d:18:3" % a, "S%d:6:48:8" % a, 1.0 / 6, "cq:%d:%d" % (a, a + 1), mul, add, sem="l2r")
-    tt("dtab:9:15", "cnt:%d:72:8" % (24 + R), "cnt:%d:%d:8" % (15 + R, 56 + R), sub, sem="du")
+    ts("px", "kd", "c1", "F4:1:2", add, sub, sem="pl")
     need("l2r")
-    need("q1c", 1)
+    need("q1c")
     need("gd", 32)
-    need("rc1", arrivals(False))
-    pickc("land2", 240 * R, 240 * R + OUT, "land1", W1 + 1, "l2", 0, 18, "q2c")
-    need("w_in")
-    v(V.quantize_mx, "qw", [], T.sw[:], T.ws[:], sem="qwr")
+    need("rc1", arrive2)
+    for a, b in runs2:
+        pickc("land2", mine + 16 * (a - 3 * R), mine + 16 * (b - 3 * R), "land1", W1 + 1, "l2", a, b, "q2c")
 
+    need(*own)
+    need(*pad)
+    last.pop("Xin")
+    need("rx", arrive2)
+    cp("XR:0:64", "Xin:0:64@px:0:4")
+    ts("t2", "F4:3:4", -32.0 / 9, 64.0 / 9, mul, add)
     scan("MX", "DR", "XR", add, O.max)
+    ts("t3", "eh2", "t2", 2.0, mul, add)
     need(*made.pop("Db"))
-    ts("Db:0:32:2", "MX:7:128:8", 1.0 / 6, None, mul)
+    ts("Db:0:32:2", "MX:7:128:8", 1.0 / 6, LIFT - 2.5 / 6, mul, add)
     cp("Db:1:32:4", "MX:6:128:16")
+    ts("lc2:0:1", "F4:5:6", 4.0, "t3", mul, add)
     scan("Y3:0:32", "hv", "Db", mul, add)
-    tr("YY:0:32", "Y3:0:32")
-    tr("YY:32:64", "Y3:0:32")
-    tr("Y3:32:64", "YY:16:48")
-    ts("l3", "Y3:0:64@lc2:0:1", OUT * 780.0 - 130, None, add, sem="l3r")
+    need("w_in")
+    inc(V.quantize_mx(T.qw[:, 0:128], T.sw[:, 0:128], T.ws[:, 0:512]), "qwr")
+    tr("val:16:48", "Y3:0:32")
+    tr("Y3:32:96", "val")
+    ts("l3", "Y3:0:96@lc2:0:1", (6.0 * OUT - 1) * LIFT, None, add, sem="l3r")
     need("l3r")
     need("q2c")
-    need("rc2", arrivals(False))
+    need("rc2", arrive2)
     for h in range(2):
         pickc("q3", 128 * h, 128 * h + 128, "land2", W2, "l3", 8 * h, 8 * h + 8, "q3c%d" % h)
+        if h == 0:
+            inc(V.quantize_mx(T.qw[:, 128:256], T.sw[:, 128:256], T.ws[:, 512:1024]), "qwr")
 
     def part(o, h):
         return slice(256 * o + 128 * h, 256 * o + 128 * h + 128), slice(512 * (2 * o + h), 512 * (2 * o + h) + 128)
@@ -333,11 +391,12 @@ def rank_program(g, core, T, topo):
         need("mm%d%d" % (o, h), 1)
         inc(V.tensor_copy(T.ys[:, y], T.ps[:, p]), "y%d%d" % (o, h))
 
-    w(E, "qwr", 1)
     for h in range(2):
         w(E, "q3c%d" % h, 1)
         w(E, "q3s%d" % h, 1)
         for o in ((0, 1), (1, 0))[h]:
+            if h == 0:
+                w(E, "qwr", o + 1)
             inc(E.matmul_mx(T.ps[:, part(o, h)[1]], T.qw[:, 128 * o:128 * o + 128], T.sw[:, 128 * o:128 * o + 128],
                             T.q3[:, 128 * h:128 * h + 128], T.s3[:, 128 * h:128 * h + 128], True, True), "mm%d%d" % (o, h))
     y, p = part(1, 1)
@@ -346,25 +405,5 @@ def rank_program(g, core, T, topo):
     for q, o, h in ((S, 0, 0), (S, 1, 0), (S, 0, 1), (A, 1, 1)):
         w(q, "y%d%d" % (o, h), 1)
         inc(q.dma_start(T.y[:, part(o, h)[0]], T.ys[:, part(o, h)[0]]), "st", 16)
-
-    w(g, "sb", 1)
-    others = [topo.addr(c) for c in cores if c != core]
-    tot["ls"] = len(common(core))
-    g.remote_dma_fused([RemoteDMATransfer(dst_ids=[DstId(rid=a[0], pnc=a[1]) for a in others], remote_sem=T.sem.rc,
-                                          dma_engine_mask=sum(1 << e for e in common(core)), srcs=[T.Sb[:, 0:8]],
-                                          dsts=[T.cnt[:, 8 * R + 16:8 * R + 24] for a in others])], local_sem=T.sem.ls)
-    w(g, "q1c", 1)
-    fused(lambda d: T.land1[:, 48 * d:48 * d + C1].bitcast(dt.uint8),
-          lambda d: T.land1[:, base1(R, d):base1(R, d) + C1].bitcast(dt.uint8), "rc1", False)
-    w(g, "q1s", 1)
-    fused(lambda d: T.lans1[:, 48 * d:48 * d + C1], lambda d: T.lans1[:, base1(R, d):base1(R, d) + C1], "rs1", True)
-    w(g, "xsr", 1)
-    fused(lambda d: T.Xs[:, 8 * d:8 * d + 8], lambda d: T.Xin[:, 8 * R:8 * R + 8], "rx", False)
-    mine = 240 * R
-    w(g, "q2c", 1)
-    fused(lambda d: T.land2[:, mine + 48 * d:mine + 48 * d + C2].bitcast(dt.uint8),
-          lambda d: T.land2[:, OUT * R:OUT * R + C2].bitcast(dt.uint8), "rc2", False)
-    w(g, "q2s", 1)
-    fused(lambda d: T.lans2[:, mine + 48 * d:mine + 48 * d + C2], lambda d: T.lans2[:, OUT * R:OUT * R + C2], "rs2", True)
-    for s in ("v", "ls", "st", "gi", "ac"):
+    for s in ("v", "gi", "ac", "ls", "st"):
         w(g, s, tot[s])

@@ -6,18 +6,18 @@ C1, C2 = 43, 48
 HEAD = 272
 W1 = HEAD + 5 * C1
 OUT = 6 * C2
-W2 = 6 * OUT
+W2 = 5 * OUT + C2
 FAR = 4096
 LIFT = 130
 _C = "float8_e4m3fn_x4"
 _BUFS = {
-    "int32": "toh 8 p8 8 Dc 48 I4 6 P6 8",
-    "uint16": "repa 4 pm 4 lc 2 lc2 2 tou 8 Pu 8 off1 8 l1 32 l2 36 l3 16 px 8 pd 8 pg 4",
+    "int32": "toh 8 p8 8 Dc 48 I4 6",
+    "uint16": "repa 4 pm 4 lc 2 lc2 2 tou 8 Pu 8 off1 8 l1 32 l2 18 l3 16 pg 4",
     "bfloat16": "xs 1024 ws 1024 cval 128 idt 256 SbT 32 Sb 32 win1 304 TR 576 Pf 128 keywin 1536 trk 1536 "
-                "Xin 112 cnt 80 Db 32",
-    "float32": "cvr 128 F4 6 hf 1 c1 1 eh 1 eg 1 eh2 1 pv 1 cq 3 k8 2 kd 8 KP 64 LC 64 M 64 CT 64 Cb 272 "
-               "B3 97 QQ 100 val 64 PP 64 Pq 8 e1 8 Y1 18 G 64 bf 48 DN 48 NG0 48 NG1 48 NG2 48 S0 48 S1 48 S2 48 "
-               "dtab 16 DR 128 XR 128 MX 128 hv 32 Y3 96 t2 1 t3 1 ys 512",
+                "Xin 112 cnt 80 Db 32 P6 64",
+    "float32": "cvr 128 F4 6 hf 1 c1 1 eh 1 eg 1 pv 1 cq 3 k8 2 kd 8 KP 64 LC 64 M 64 CT 64 Cb 272 "
+               "B3 97 QQ 100 val 64 PP 64 M6 64 e1 8 Y1 18 G 64 bf 48 DN 48 NG0 48 NG1 48 NG2 48 S0 48 S1 48 S2 48 "
+               "dtab 16 DR 64 DX 64 XR 64 MX 64 MU 64 hv 32 Y3 96 t2 2 t3 1 ys 512",
     _C: "qx 256 qw 256 land1 512 land2 %d q3 256" % W2,
     "uint8": "sx 256 sw 256 lans1 512 lans2 %d s3 256" % W2,
 }
@@ -26,38 +26,17 @@ for _d, _s in _BUFS.items():
     _p = _s.split()
     for _n, _w in zip(_p[0::2], _p[1::2]):
         SCRATCH[_n] = ("sbuf", [128, int(_w)], _d)
-SEMAPHORES = ("v gi to_in x_in w_in zr w0 f4r ac le cd sb p_ok l1r qxr gd q1c q1s xsr du pl l2r l2d q2c q2s "
+SEMAPHORES = ("v gi to_in x_in w_in zr w0 f4r ac le cd sb p_ok l1r qxr gd q1c q1s xsr l2r q2c q2s "
               "l3r qwr q3c0 q3c1 q3s0 q3s1 mm00 mm01 mm10 mm11 y00 y01 y10 y11 st rc rx rc1 rs1 rc2 rs2 ls").split()
 
 
-def _shares(src, cores, topo, flip):
-    k = cores.index(src)
-    ds = sorted(cores[k + 1:] + cores[:k], key=lambda c: topo.die(c) == topo.die(src))
-    e = topo.engines(src, ds[0])
-    e = e[0::2] + e[1::2]
-    h, w = len(e) // 2, len(e) // 8
-    if flip:
-        e = e[h:] + e[:h]
-    return {c: e[h + (i - 1) * w:h + i * w] if i else e[:h] for i, c in enumerate(ds)}
-
-
-def _even(src, cores, topo):
+def _deal(src, cores, topo):
     k = cores.index(src)
     ds = sorted(cores[k + 1:] + cores[:k], key=lambda c: (c == cores[k ^ 1], topo.die(c) == topo.die(src)))
     e = topo.engines(src, ds[0])
     e = e[0::2] + e[1::2]
     w = len(e) // 4
     return {c: e[i * w:(i + 1) * w] for i, c in enumerate(ds[:4])}, {ds[4]: e}
-
-
-def _halves(src, cores, topo):
-    h = cores.index(src) // 3
-    far, near = cores[3 - 3 * h:6 - 3 * h], [c for c in cores[3 * h:3 * h + 3] if c != src]
-    far = sorted(far, key=lambda c: topo.die(c) == topo.die(src))
-    e = topo.engines(src, far[0])
-    e = e[0::2] + e[1::2]
-    q = len(e) // 4
-    return {far[0]: e[:2 * q], far[1]: e[2 * q:3 * q], far[2]: e[3 * q:]}, {near[0]: e[:2 * q], near[1]: e[2 * q:]}
 
 
 def rank_program(g, core, T, topo):
@@ -123,26 +102,35 @@ def rank_program(g, core, T, topo):
     def tr(out, i, **k):
         v(V.transpose, out, [i], **k)
 
+    def quantise(t, h):
+        a, b = 128 * h, 128 * h + 128
+        inc(V.quantize_mx(T["q" + t][:, a:b], T["s" + t][:, a:b], T[t + "s"][:, 4 * a:4 * b]), "q%sr" % t)
+
+    def pickc(out, a, b, src, n, lst, c, e, sem):
+        inc(V.tensor_copy(T[out][:, a:b].bitcast(dt.uint32), T[src][:, 0:n].bitcast(dt.uint32).indirect(T[lst][:, c:e])), sem)
+
+    def picks(out, a, b, src, n, lst, c, e, sem):
+        inc(A.activation(T[out][:, a:b], T[src][:, 0:n].indirect(T[lst][:, c:e]), AF.Copy), sem)
+
     def base1(r, m):
         return C1 * m if r == m else HEAD + C1 * [k for k in range(N) if k != m].index(r)
 
-    arrivals = sum(len(_shares(c, cores, topo, False)[core]) for c in cores if c != core)
+    arrivals = sum(len(sh.get(core, [])) for c in cores if c != core for sh in _deal(c, cores, topo))
 
-    arrive2 = sum(len(sh.get(core, [])) for c in cores if c != core for sh in _even(c, cores, topo))
-
-    def exchange(buf, at, to, n, sem, flip, sh=None):
-        sh = sh or _shares(core, cores, topo, flip)
-        t = []
-        for c in sh:
-            rid, pid, _ = topo.addr(c)
-            d = cores.index(c)
-            src, dst = T[buf][:, at(d):at(d) + n], T[buf][:, to(d):to(d) + n]
-            if SCRATCH[buf][2] == _C:
-                src, dst = src.bitcast(dt.uint8), dst.bitcast(dt.uint8)
-            t.append(RemoteDMATransfer(dst_ids=[DstId(rid=rid, pnc=pid)], dma_engine_mask=sum(1 << e for e in sh[c]),
-                                       remote_sem=T.sem[sem], src=src, dst=dst))
-            tot["ls"] += len(sh[c])
-        g.remote_dma_fused(t, local_sem=T.sem.ls)
+    def exchange(buf, at, to, n, sem, ready, counts):
+        for sh, k in zip(_deal(core, cores, topo), counts):
+            w(g, ready, k)
+            t = []
+            for c in sh:
+                rid, pid, _ = topo.addr(c)
+                d = cores.index(c)
+                src, dst = T[buf][:, at(d):at(d) + n], T[buf][:, to(d):to(d) + n]
+                if SCRATCH[buf][2] == _C:
+                    src, dst = src.bitcast(dt.uint8), dst.bitcast(dt.uint8)
+                t.append(RemoteDMATransfer(dst_ids=[DstId(rid=rid, pnc=pid)], dma_engine_mask=sum(1 << e for e in sh[c]),
+                                           remote_sem=T.sem[sem], src=src, dst=dst))
+                tot["ls"] += len(sh[c])
+            g.remote_dma_fused(t, local_sem=T.sem.ls)
 
     def common(c):
         o = [k for k in cores if k != c]
@@ -170,10 +158,8 @@ def rank_program(g, core, T, topo):
     iota("cvr", [[16, 8], [1, 8], [128, 2]])
     iota("k8", [[8, 2]])
     iota("idt", [[1, 256]])
-    lam = [-298] + [6 * base1(r, R) for r in range(N)] + [33.5 + R]
-    for k in range(3):
-        iota("KP:%d:64:8" % k, [[-6 if k else 298, 8]], lam[k])
-    ramps = made.pop("KP")
+    iota("keywin:1216:1536", [[0, 320]], -FAR)
+    filled = made.pop("keywin")
     w(g, "sb", 1)
     others = [topo.addr(c) for c in cores if c != core]
     tot["ls"] = len(common(core))
@@ -181,25 +167,21 @@ def rank_program(g, core, T, topo):
                                           dma_engine_mask=sum(1 << e for e in common(core)), srcs=[T.Sb[:, 0:8]],
                                           dsts=[T.cnt[:, 8 * R + 16:8 * R + 24] for a in others])], local_sem=T.sem.ls)
     sizes = sum(len(common(c)) for c in cores if c != core)
-    mine = OUT * R
+    iota("dtab:1:8", [[0, 7]], 6)
+    iota("dtab:15:16", [[0, 1]], 42)
     iota("Xin:48:64", [[0, 16]], -FAR)
     pad = made.pop("Xin")
     iota("hv:0:32:2", [[0, 8], [OUT, 2]])
     iota("hv:1:32:2", [[0, 8], [7, 2]], -6)
+    for buf, sem, ready in (("land1", "rc1", "q1c"), ("lans1", "rs1", "q1s")):
+        exchange(buf, lambda d: C1 * d, lambda d: base1(R, d), C1, sem, ready, (1, 1))
+    exchange("Xin", lambda d: 64 + 8 * d, lambda d: 8 * R, 8, "rx", "xsr", (1, 1))
     iota("Db:3:32:4", [[0, 8]])
-    for buf, ready, sem in (("lans1", "q1s", "rs1"), ("land1", "q1c", "rc1")):
-        w(g, ready, 1)
-        for sh in _even(core, cores, topo):
-            exchange(buf, lambda d: C1 * d, lambda d: base1(R, d), C1, sem, False, sh)
-    w(g, "xsr", 1)
-    for sh in _even(core, cores, topo):
-        exchange("Xin", lambda d: 64 + 8 * d, lambda d: 8 * R, 8, "rx", False, sh)
-    for buf, ready, sem in (("land2", "q2c", "rc2"), ("lans2", "q2s", "rs2")):
-        w(g, ready, 1)
-        for sh in _even(core, cores, topo):
-            exchange(buf, lambda d: mine + C2 * (d - R), lambda d: mine, C2, sem, False, sh)
-    runs1 = ((0, 17),)
-    runs2 = ((0, 18),)
+    mine = (OUT - C2) * R
+    pair = 6 * (R // 2)
+    runs = [r for r in ((0, pair), (pair + 6, 18), (pair, pair + 6)) if r[0] < r[1]]
+    for buf, sem, ready in (("land2", "rc2", "q2c"), ("lans2", "rs2", "q2s")):
+        exchange(buf, lambda d: mine + C2 * d, lambda d: OUT * R, C2, sem, ready, (len(runs) - 1, len(runs)))
 
     def act(out, i, sem="ac", f=AF.Copy, **k):
         inc(A.activation(ap(out), ap(i), f, **k), sem)
@@ -210,71 +192,69 @@ def rank_program(g, core, T, topo):
         f = [int(i) for i in out.split(":")[1:]]
         act(out, "B3:0:%d" % len(range(*f)), bias=c)
 
-    def picks(out, a, b, src, n, lst, c, e, sem):
-        inc(A.activation(T[out][:, a:b], T[src][:, 0:n].indirect(T[lst][:, c:e]), AF.Copy), sem)
-
     w(A, "zr", 1)
     for b in ("LC:0:16", "Cb:71:272:8", "Cb:0:16"):
         const(b)
     made.pop("LC")
     w(A, "w0", 1)
     act("keywin:0:304", "win1", bias=-float(FAR))
-    made["win1"] = made["keywin"]
     w(A, "f4r", 1)
     act("hf", "F4:3:4", scale=8.0)
+    act("keywin:304:608", "win1", bias=-float(FAR))
+    made["win1"] = made["keywin"]
     w(A, "ac", made["hf"][1])
-    act("keywin:304:576", "keywin:0:272")
-    w(A, "le", 2)
+    w(A, "le", 3)
     act("M", "LC:0:64@pm")
     w(A, "cd", 1)
-    act("CT", "Cb:0:64@pm")
+    lift = 6 * LIFT - 2.5
+    act("CT", "Cb:0:64@pm", bias=-lift)
+    act("M6", "LC:0:64@pm")
     w(A, "ac", made["M"][1])
     const("M:7:64:8", 43.0 / 257)
+    w(A, "ac", made["M6"][1])
+    const("M6:7:64:8", 1.0 / 6)
     w(A, "gi", made["cvr"][1])
     act("cval", "cvr", f=AF.Identity, bias=ap("hf"))
-    w(A, "ac", made["keywin"][1])
-    act("keywin:576:1152", "keywin:0:576")
-    act("keywin:1152:1536", "keywin:0:384")
+    act("keywin:608:1216", "keywin:0:608")
     w(A, "p_ok", 1)
     w(A, "gi", made["idt"][1])
     act("Pf", "idt:0:256@Pu:0:8")
+    lam = [-298.0] + [6.0 * base1(r, R) for r in range(N)] + [33.5 + R]
+    for k in range(8):
+        act("KP:%d:64:8" % k, "kd", bias=lam[k], scale=-6.0 if k else 298.0)
     w(A, "sb", 1)
     act("cnt:%d:%d" % (8 * R + 16, 8 * R + 24), "Sb:0:8")
     const("cnt:0:16", 256.0)
     const("cnt:64:80", 256.0)
-    for k in range(3, 8):
-        act("KP:%d:64:8" % k, "kd", bias=float(lam[k]), scale=-6.0)
+    const("dtab:0:9:8", -4.0 * FAR)
     w(A, "qxr", 2)
     w(A, "l1r", 1)
-    for a, b in runs1:
-        picks("lans1", 16 * a, 16 * b, "sx", 256, "l1", a, b, "q1s")
-    const("dtab:0:9:8", -4.0 * FAR)
-    const("dtab:1:8", 6.0)
-    const("dtab:15:16", 42.0)
-    w(A, "ac", made["cnt"][1])
+    picks("lans1", 0, HEAD, "sx", 256, "l1", 0, 17, "q1s")
+    act("t2:0:1", "F4:3:4", scale=32.0 / 9, bias=-64.0 / 9)
+    act("t2:1:2", "F4:3:4", scale=-32.0, bias=66.0)
+    w(A, "ac", made["dtab"][1])
+    w(A, *pad)
+    act("DX", "dtab:0:8@repa", bias=-6.0)
     w(A, "rc", sizes)
     for t in range(1, 7):
         act("dtab:%d:%d" % (8 + t, 9 + t), "cnt:%d:%d" % (7 + 8 * t + R, 8 + 8 * t + R), f=AF.Identity, scale=-1.0,
             bias=ap("cnt:%d:%d" % (16 + 8 * t + R, 17 + 8 * t + R)))
-    w(A, "pl", 1)
-    w(A, "ac", made["dtab"][1])
-    act("DR", "dtab:0:16@pd", bias=-6.0)
     w(A, "xsr", 1)
     act("Xin:%d:%d" % (8 * R, 8 * R + 8), "Xin:%d:%d" % (64 + 8 * R, 72 + 8 * R))
-    w(A, "l2r", 3)
+    w(A, "ac", made["dtab"][1])
+    act("DR", "dtab:8:16@repa", bias=-6.0)
+    w(A, "ac", made.pop("Xin")[1])
     w(A, "q1s", 1)
     w(A, "gd", 32)
-    w(A, "rs1", arrive2)
-    for a, b in runs2:
-        picks("lans2", mine + 16 * (a - 3 * R), mine + 16 * (b - 3 * R), "lans1", W1 + 1, "l2", a, b, "q2s")
-    w(A, "ac", tot["ac"])
-    w(A, *pad)
-    w(A, "pl", 2)
-    w(A, "rx", arrive2)
-    act("XR:64:128", "Xin:0:64@px:4:8")
+    w(A, "rx", arrivals)
+    act("XR", "Xin:0:64@pm")
+    w(A, "rs1", arrivals)
+    w(A, "l2r", 3)
+    for a, b in runs:
+        picks("lans2", mine + 16 * a, mine + 16 * b, "lans1", W1 + 1, "l2", a, b, "q2s")
     w(A, "l3r", 1)
-    w(A, "q2s", 1)
-    w(A, "rs2", arrive2)
+    w(A, "q2s", len(runs))
+    w(A, "rs2", arrivals)
     for h in range(2):
         picks("s3", 128 * h, 128 * h + 128, "lans2", W2, "l3", 8 * h, 8 * h + 8, "q3s%d" % h)
 
@@ -287,17 +267,18 @@ def rank_program(g, core, T, topo):
     ts("I4:4:5", "p8:4:5", 1, None, band)
     ts("I4:5:6", "p8:5:6", 1, 7, shr, band)
     cp("F4", "I4", sem="f4r")
-    ts("repa", "B3:0:4", "F4:0:1", None, add)
     ts("c1", "F4:0:1", 8.0, "F4:1:2", mul, add)
-    ts("pd", "B3:0:8", "F4:2:3", None, add, sem="pl")
+    ts("repa", "B3:0:4", "F4:0:1", None, add, sem="le")
+    ts("cq", "kd:0:3", 16.0, "F4:2:3", mul, add)
     ts("pm", "kd:0:4", 2.0, "c1", mul, add, sem="le")
+    ts("eh", "F4:4:5", "F4:3:4", 9.0, O.is_equal, mul)
 
     need("to_in")
     tt("LC:16:64", "toh:0:8@repa:0:3", "Dc", O.is_lt, sem="le")
     cp("tou", "toh")
     need(*made.pop("Cb"))
     scan("Cb:16:64", "LC:16:64", "LC:8:56", add, sub, sem="cd")
-    ts("eh", "F4:4:5", "F4:3:4", 9.0, O.is_equal, mul)
+    ts("pg", "pm", 7.0, None, add)
     tr("B3:65:97", "Cb:23:272:8")
     tr("B3:32:64", "Cb:15:264:8")
     ts("eg", "F4:4:5", "F4:3:4", "F4:5:6", O.is_gt, add)
@@ -309,37 +290,30 @@ def rank_program(g, core, T, topo):
     tt("val", "QQ:64:72@repa", "CT", sub)
     tr("Sb", "SbT", sem="sb")
     scan("PP", "val", "M", O.max, mul)
+    scan("P6", "val", "M6", O.max, mul)
+    ts("Pu", "PP:7:64:8", 257.0 / 43, -lift, mul, add, sem="p_ok")
+    tt("e1", "P6:7:64:8", "PP:7:64:8", sub)
     ts("lc", "k8", "pv", 17.0, add, O.min)
-    ts("P6", "PP:7:64:8", 257.0 / 258, -2.5 / 6, mul, add)
-    ts("Pu", "PP:7:64:8", 257.0 / 43, None, mul, sem="p_ok")
-    tt("e1", "P6", "PP:7:64:8", sub)
-    ts("eh2", "eh", -1.0, 9.0, mul, add)
-    ts("off1", "e1", -257.0, 16.0, mul, add)
-    ts("pg", "pm", 7.0, None, add)
-    cp("win1:0:304@off1:0:8", "cval")
+    ts("off1", "e1", -257.0, 16 + 257 * LIFT - 43 * lift, mul, add)
     need("x_in")
-    inc(V.quantize_mx(T.qx[:, 0:128], T.sx[:, 0:128], T.xs[:, 0:512]), "qxr")
+    quantise("x", 0)
+    cp("win1:0:304@off1:0:8", "cval")
+    need(*filled)
+    cp("keywin:0:1536@tou:0:8", "Pf")
     tr("TR:0:288", "win1:0:288")
     tr("TR:288:576", "win1:16:304")
-    inc(V.quantize_mx(T.qx[:, 128:256], T.sx[:, 128:256], T.xs[:, 512:1024]), "qxr")
+    quantise("x", 1)
     tt("Y1", "TR:0:576:32", "TR:16:576:32", add)
-    ts("cq", "kd:0:3", 16.0, "F4:2:3", mul, add)
+    tr("trk:0:224", "keywin:0:224")
     cp("l1", "Y1@lc", sem="l1r")
-    cp("keywin:0:1536@tou:0:8", "Pf")
+    tr("trk:224:448", "keywin:224:448")
     need("qxr")
     need("l1r")
+    pickc("land1", 0, HEAD, "qx", 256, "l1", 0, 17, "q1c")
+    tr("trk:448:1536", "keywin:448:1536")
 
-    def pickc(out, a, b, src, n, lst, c, e, sem):
-        inc(V.tensor_copy(T[out][:, a:b].bitcast(dt.uint32), T[src][:, 0:n].bitcast(dt.uint32).indirect(T[lst][:, c:e])), sem)
-
-    for a, b in runs1:
-        pickc("land1", 16 * a, 16 * b, "qx", 256, "l1", a, b, "q1c")
-
-    tr("trk", "keywin")
-    need(*ramps)
     need("rc", sizes)
     tt("G", "cnt@pg", "KP", add)
-    own = made.pop("Xin")
     tt("Xin:64:112", "trk:0:1536:32", "trk:16:1536:32", O.max, sem="xsr")
     scan("bf", "G:0:48", "G:8:56", add, sub, 298 - 5.5)
     tt("DN", "G:0:48", "G:9:57", sub)
@@ -349,39 +323,34 @@ def rank_program(g, core, T, topo):
         scan("S%d" % a, "DN", "NG%d" % a, add, mul)
     for a in range(3):
         ts("l2:%d:18:3" % a, "S%d:6:48:8" % a, 1.0 / 6, "cq:%d:%d" % (a, a + 1), mul, add, sem="l2r")
-    ts("px", "kd", "c1", "F4:1:2", add, sub, sem="pl")
+    ts("t3", "eh", "t2:0:1", "t2:1:2", mul, add)
     need("l2r")
     need("q1c")
     need("gd", 32)
-    need("rc1", arrive2)
-    for a, b in runs2:
-        pickc("land2", mine + 16 * (a - 3 * R), mine + 16 * (b - 3 * R), "land1", W1 + 1, "l2", a, b, "q2c")
+    need("rc1", arrivals)
 
-    need(*own)
-    need(*pad)
-    last.pop("Xin")
-    need("rx", arrive2)
-    cp("XR:0:64", "Xin:0:64@px:0:4")
-    ts("t2", "F4:3:4", -32.0 / 9, 64.0 / 9, mul, add)
-    scan("MX", "DR", "XR", add, O.max)
-    ts("t3", "eh2", "t2", 2.0, mul, add)
+    for a, b in runs:
+        pickc("land2", mine + 16 * a, mine + 16 * b, "land1", W1 + 1, "l2", a, b, "q2c")
+    scan("MX", "DX", "XR", add, O.max)
+    scan("MU", "DR", "XR", add, O.max)
     need(*made.pop("Db"))
-    ts("Db:0:32:2", "MX:7:128:8", 1.0 / 6, LIFT - 2.5 / 6, mul, add)
-    cp("Db:1:32:4", "MX:6:128:16")
+    ts("Db:0:32:4", "MX:7:64:8", 1.0 / 6, LIFT - 2.5 / 6, mul, add)
+    cp("Db:1:32:4", "MX:7:64:8")
+    ts("Db:2:32:4", "MU:7:64:8", 1.0 / 6, LIFT - 2.5 / 6, mul, add)
     ts("lc2:0:1", "F4:5:6", 4.0, "t3", mul, add)
     scan("Y3:0:32", "hv", "Db", mul, add)
     need("w_in")
-    inc(V.quantize_mx(T.qw[:, 0:128], T.sw[:, 0:128], T.ws[:, 0:512]), "qwr")
+    quantise("w", 0)
     tr("val:16:48", "Y3:0:32")
     tr("Y3:32:96", "val")
     ts("l3", "Y3:0:96@lc2:0:1", (6.0 * OUT - 1) * LIFT, None, add, sem="l3r")
     need("l3r")
     need("q2c")
-    need("rc2", arrive2)
+    need("rc2", arrivals)
     for h in range(2):
         pickc("q3", 128 * h, 128 * h + 128, "land2", W2, "l3", 8 * h, 8 * h + 8, "q3c%d" % h)
         if h == 0:
-            inc(V.quantize_mx(T.qw[:, 128:256], T.sw[:, 128:256], T.ws[:, 512:1024]), "qwr")
+            quantise("w", 1)
 
     def part(o, h):
         return slice(256 * o + 128 * h, 256 * o + 128 * h + 128), slice(512 * (2 * o + h), 512 * (2 * o + h) + 128)

from concourse.bass import DstId, RemoteDMATransfer
from concourse.mybir import dt, AluOpType, ActivationFunctionType

N = 6
C1, C2 = 43, 48
HEAD = 272
W1 = HEAD + 5 * C1
OUT = 6 * C2
W2 = 5 * OUT + C2
FAR = 4096
LIFT = 130
_C = "float8_e4m3fn_x4"
_BUFS = {
    "int32": "toh 8 p8 8 Dc 48 I4 6",
    "uint16": "repa 4 pm 4 lc 2 lc2 2 tou 8 Pu 8 off1 8 l1 32 l2 18 l3 16 pg 4",
    "bfloat16": "xs 1024 ws 1024 cval 128 idt 256 SbT 32 Sb 32 win1 304 TR 576 Pf 128 keywin 1536 trk 1536 "
                "Xin 112 cnt 80 Db 32 P6 64",
    "float32": "cvr 128 F4 6 hf 1 c1 1 eh 1 eg 1 pv 1 cq 3 k8 2 kd 8 KP 64 LC 64 M 64 CT 64 Cb 272 "
               "B3 97 QQ 100 val 64 PP 64 M6 64 e1 8 Y1 18 G 64 bf 48 DN 48 NG0 48 NG1 48 NG2 48 S0 48 S1 48 S2 48 "
               "dtab 16 DR 64 DX 64 XR 64 MX 64 MU 64 hv 32 Y3 96 t2 2 t3 1 ys 512",
    _C: "qx 256 qw 256 land1 512 land2 %d q3 256" % W2,
    "uint8": "sx 256 sw 256 lans1 512 lans2 %d s3 256" % W2,
}
SCRATCH = {"ps": ("psum", [128, 2048], "float32")}
for _d, _s in _BUFS.items():
    _p = _s.split()
    for _n, _w in zip(_p[0::2], _p[1::2]):
        SCRATCH[_n] = ("sbuf", [128, int(_w)], _d)
SEMAPHORES = ("v gi to_in x_in w_in zr w0 f4r ac le cd sb p_ok l1r qxr gd q1c q1s xsr l2r q2c q2s "
              "l3r qwr q3c0 q3c1 q3s0 q3s1 mm00 mm01 mm10 mm11 y00 y01 y10 y11 st rc rx rc1 rs1 rc2 rs2 ls").split()


def _deal(src, cores, topo):
    k = cores.index(src)
    ds = sorted(cores[k + 1:] + cores[:k], key=lambda c: (c == cores[k ^ 1], topo.die(c) == topo.die(src)))
    e = topo.engines(src, ds[0])
    e = e[0::2] + e[1::2]
    w = len(e) // 4
    return {c: e[i * w:(i + 1) * w] for i, c in enumerate(ds[:4])}, {ds[4]: e}


def rank_program(g, core, T, topo):
    R = T.rank_of(core)
    if R is None:
        return
    cores = list(T.cores)
    V, A, S, E = g.vector, g.scalar, g.sync, g.tensor
    O = AluOpType
    add, sub, mul = O.add, O.subtract, O.mult
    shr, band = O.arith_shift_right, O.bitwise_and
    AF = ActivationFunctionType
    tot, last, waited = {}, {}, {}
    made = {}

    def inc(inst, sem, n=1):
        inst.then_inc(T.sem[sem], n)
        tot[sem] = tot.get(sem, 0) + n

    def need(sem, n=None):
        n = tot[sem] if n is None else n
        if waited.get(sem, 0) < n:
            waited[sem] = n
            V.wait_ge(T.sem[sem], n)

    def w(q, sem, n):
        q.wait_ge(T.sem[sem], n)

    def ap(s):
        s, _, off = s.partition("@")
        f = s.split(":")
        a = T[f[0]][:, slice(*[int(i) for i in f[1:]])] if f[1:] else T[f[0]][:]
        return a.indirect(ap(off)) if off else a

    def reads(s):
        for n in s.replace("@", ":").split(":"):
            if n in made:
                need(*made[n])
            if n in last:
                need(*last[n])

    def v(call, out, ins, *more, sem="v"):
        for s in ins + ([out] if "@" in out else []):
            reads(s)
        inc(call(ap(out), *[ap(s) for s in ins], *more), sem)
        last[out.split(":")[0].split("@")[0]] = (sem, tot[sem])

    def ts(out, i, s1, s2, *ops, **k):
        for s in (s1, s2):
            if isinstance(s, str):
                reads(s)
        v(V.tensor_scalar, out, [i], *[ap(s) if isinstance(s, str) else s for s in (s1, s2)], *ops, **k)

    def tt(out, i, j, op, **k):
        v(V.tensor_tensor, out, [i, j], op, **k)

    def cp(out, i, **k):
        v(V.tensor_copy, out, [i], **k)

    def scan(out, i, j, op0, op1, first=0.0, **k):
        v(V.tensor_tensor_scan, out, [i, j], first, op0, op1, **k)

    def tr(out, i, **k):
        v(V.transpose, out, [i], **k)

    def quantise(t, h):
        a, b = 128 * h, 128 * h + 128
        inc(V.quantize_mx(T["q" + t][:, a:b], T["s" + t][:, a:b], T[t + "s"][:, 4 * a:4 * b]), "q%sr" % t)

    def pickc(out, a, b, src, n, lst, c, e, sem):
        inc(V.tensor_copy(T[out][:, a:b].bitcast(dt.uint32), T[src][:, 0:n].bitcast(dt.uint32).indirect(T[lst][:, c:e])), sem)

    def picks(out, a, b, src, n, lst, c, e, sem):
        inc(A.activation(T[out][:, a:b], T[src][:, 0:n].indirect(T[lst][:, c:e]), AF.Copy), sem)

    def base1(r, m):
        return C1 * m if r == m else HEAD + C1 * [k for k in range(N) if k != m].index(r)

    arrivals = sum(len(sh.get(core, [])) for c in cores if c != core for sh in _deal(c, cores, topo))

    def exchange(buf, at, to, n, sem, ready, counts):
        for sh, k in zip(_deal(core, cores, topo), counts):
            w(g, ready, k)
            t = []
            for c in sh:
                rid, pid, _ = topo.addr(c)
                d = cores.index(c)
                src, dst = T[buf][:, at(d):at(d) + n], T[buf][:, to(d):to(d) + n]
                if SCRATCH[buf][2] == _C:
                    src, dst = src.bitcast(dt.uint8), dst.bitcast(dt.uint8)
                t.append(RemoteDMATransfer(dst_ids=[DstId(rid=rid, pnc=pid)], dma_engine_mask=sum(1 << e for e in sh[c]),
                                           remote_sem=T.sem[sem], src=src, dst=dst))
                tot["ls"] += len(sh[c])
            g.remote_dma_fused(t, local_sem=T.sem.ls)

    def common(c):
        o = [k for k in cores if k != c]
        return [e for e in topo.engines(c, o[0]) if all(e in topo.engines(c, k) for k in o)]

    for b in range(4):
        inc((S, A)[b % 2].dma_start(T.toh[32 * b:32 * b + 32, :], T.to[:, :]), "to_in", 16)
    inc(S.dma_start(T.xs[:, 0:512], T.x[:, 0:512]), "x_in", 16)
    inc(A.dma_start(T.xs[:, 512:1024], T.x[:, 512:1024]), "x_in", 16)
    w(S, "x_in", 32)
    inc(S.dma_start(T.ws[:], T.w[:]), "w_in", 16)
    w(S, "qxr", 2)
    inc(S.dma_start(T.land1[:, W1:W1 + 1].bitcast(dt.uint8), T.qx[:, 0:1].bitcast(dt.uint8)), "gd", 16)
    inc(S.dma_start(T.lans1[:, W1:W1 + 1], T.sx[:, 0:1]), "gd", 16)

    def iota(n, pat, base=0, ch=0):
        b = n.split(":")[0]
        k = {} if SCRATCH[b][2] == "int32" else {"allow_small_or_imprecise_dtypes": True}
        inc(g.iota(ap(n), pat, base, ch, **k), "gi")
        made[b] = ("gi", tot["gi"])

    iota("p8", [[0, 8]], 0, 1)
    iota("Dc", [[256, 6], [0, 8]], 256)
    iota("kd", [[1, 8]])
    iota("cvr", [[16, 8], [1, 8], [128, 2]])
    iota("k8", [[8, 2]])
    iota("idt", [[1, 256]])
    iota("keywin:1216:1536", [[0, 320]], -FAR)
    filled = made.pop("keywin")
    w(g, "sb", 1)
    others = [topo.addr(c) for c in cores if c != core]
    tot["ls"] = len(common(core))
    g.remote_dma_fused([RemoteDMATransfer(dst_ids=[DstId(rid=a[0], pnc=a[1]) for a in others], remote_sem=T.sem.rc,
                                          dma_engine_mask=sum(1 << e for e in common(core)), srcs=[T.Sb[:, 0:8]],
                                          dsts=[T.cnt[:, 8 * R + 16:8 * R + 24] for a in others])], local_sem=T.sem.ls)
    sizes = sum(len(common(c)) for c in cores if c != core)
    iota("dtab:1:8", [[0, 7]], 6)
    iota("dtab:15:16", [[0, 1]], 42)
    iota("Xin:48:64", [[0, 16]], -FAR)
    pad = made.pop("Xin")
    iota("hv:0:32:2", [[0, 8], [OUT, 2]])
    iota("hv:1:32:2", [[0, 8], [7, 2]], -6)
    for buf, sem, ready in (("land1", "rc1", "q1c"), ("lans1", "rs1", "q1s")):
        exchange(buf, lambda d: C1 * d, lambda d: base1(R, d), C1, sem, ready, (1, 1))
    exchange("Xin", lambda d: 64 + 8 * d, lambda d: 8 * R, 8, "rx", "xsr", (1, 1))
    iota("Db:3:32:4", [[0, 8]])
    mine = (OUT - C2) * R
    pair = 6 * (R // 2)
    runs = [r for r in ((0, pair), (pair + 6, 18), (pair, pair + 6)) if r[0] < r[1]]
    for buf, sem, ready in (("land2", "rc2", "q2c"), ("lans2", "rs2", "q2s")):
        exchange(buf, lambda d: mine + C2 * d, lambda d: OUT * R, C2, sem, ready, (len(runs) - 1, len(runs)))

    def act(out, i, sem="ac", f=AF.Copy, **k):
        inc(A.activation(ap(out), ap(i), f, **k), sem)
        if sem == "ac":
            made[out.split(":")[0]] = ("ac", tot["ac"])

    def const(out, c=0.0):
        f = [int(i) for i in out.split(":")[1:]]
        act(out, "B3:0:%d" % len(range(*f)), bias=c)

    w(A, "zr", 1)
    for b in ("LC:0:16", "Cb:71:272:8", "Cb:0:16"):
        const(b)
    made.pop("LC")
    w(A, "w0", 1)
    act("keywin:0:304", "win1", bias=-float(FAR))
    w(A, "f4r", 1)
    act("hf", "F4:3:4", scale=8.0)
    act("keywin:304:608", "win1", bias=-float(FAR))
    made["win1"] = made["keywin"]
    w(A, "ac", made["hf"][1])
    w(A, "le", 3)
    act("M", "LC:0:64@pm")
    w(A, "cd", 1)
    lift = 6 * LIFT - 2.5
    act("CT", "Cb:0:64@pm", bias=-lift)
    act("M6", "LC:0:64@pm")
    w(A, "ac", made["M"][1])
    const("M:7:64:8", 43.0 / 257)
    w(A, "ac", made["M6"][1])
    const("M6:7:64:8", 1.0 / 6)
    w(A, "gi", made["cvr"][1])
    act("cval", "cvr", f=AF.Identity, bias=ap("hf"))
    act("keywin:608:1216", "keywin:0:608")
    w(A, "p_ok", 1)
    w(A, "gi", made["idt"][1])
    act("Pf", "idt:0:256@Pu:0:8")
    lam = [-298.0] + [6.0 * base1(r, R) for r in range(N)] + [33.5 + R]
    for k in range(8):
        act("KP:%d:64:8" % k, "kd", bias=lam[k], scale=-6.0 if k else 298.0)
    w(A, "sb", 1)
    act("cnt:%d:%d" % (8 * R + 16, 8 * R + 24), "Sb:0:8")
    const("cnt:0:16", 256.0)
    const("cnt:64:80", 256.0)
    const("dtab:0:9:8", -4.0 * FAR)
    w(A, "qxr", 2)
    w(A, "l1r", 1)
    picks("lans1", 0, HEAD, "sx", 256, "l1", 0, 17, "q1s")
    act("t2:0:1", "F4:3:4", scale=32.0 / 9, bias=-64.0 / 9)
    act("t2:1:2", "F4:3:4", scale=-32.0, bias=66.0)
    w(A, "ac", made["dtab"][1])
    w(A, *pad)
    act("DX", "dtab:0:8@repa", bias=-6.0)
    w(A, "rc", sizes)
    for t in range(1, 7):
        act("dtab:%d:%d" % (8 + t, 9 + t), "cnt:%d:%d" % (7 + 8 * t + R, 8 + 8 * t + R), f=AF.Identity, scale=-1.0,
            bias=ap("cnt:%d:%d" % (16 + 8 * t + R, 17 + 8 * t + R)))
    w(A, "xsr", 1)
    act("Xin:%d:%d" % (8 * R, 8 * R + 8), "Xin:%d:%d" % (64 + 8 * R, 72 + 8 * R))
    w(A, "ac", made["dtab"][1])
    act("DR", "dtab:8:16@repa", bias=-6.0)
    w(A, "ac", made.pop("Xin")[1])
    w(A, "q1s", 1)
    w(A, "gd", 32)
    w(A, "rx", arrivals)
    act("XR", "Xin:0:64@pm")
    w(A, "rs1", arrivals)
    w(A, "l2r", 3)
    for a, b in runs:
        picks("lans2", mine + 16 * a, mine + 16 * b, "lans1", W1 + 1, "l2", a, b, "q2s")
    w(A, "l3r", 1)
    w(A, "q2s", len(runs))
    w(A, "rs2", arrivals)
    for h in range(2):
        picks("s3", 128 * h, 128 * h + 128, "lans2", W2, "l3", 8 * h, 8 * h + 8, "q3s%d" % h)

    v(V.memset, "B3:0:65", [], 0.0, sem="zr")
    v(V.memset, "win1", [], 0.0, sem="w0")
    ts("I4:0:1", "p8:0:1", 7, None, band)
    ts("I4:1:2", "p8:1:2", 3, 1, shr, band)
    ts("I4:2:3", "p8:2:3", 15, None, band)
    ts("I4:3:4", "p8:3:4", 4, 1, shr, band)
    ts("I4:4:5", "p8:4:5", 1, None, band)
    ts("I4:5:6", "p8:5:6", 1, 7, shr, band)
    cp("F4", "I4", sem="f4r")
    ts("c1", "F4:0:1", 8.0, "F4:1:2", mul, add)
    ts("repa", "B3:0:4", "F4:0:1", None, add, sem="le")
    ts("cq", "kd:0:3", 16.0, "F4:2:3", mul, add)
    ts("pm", "kd:0:4", 2.0, "c1", mul, add, sem="le")
    ts("eh", "F4:4:5", "F4:3:4", 9.0, O.is_equal, mul)

    need("to_in")
    tt("LC:16:64", "toh:0:8@repa:0:3", "Dc", O.is_lt, sem="le")
    cp("tou", "toh")
    need(*made.pop("Cb"))
    scan("Cb:16:64", "LC:16:64", "LC:8:56", add, sub, sem="cd")
    ts("pg", "pm", 7.0, None, add)
    tr("B3:65:97", "Cb:23:272:8")
    tr("B3:32:64", "Cb:15:264:8")
    ts("eg", "F4:4:5", "F4:3:4", "F4:5:6", O.is_gt, add)
    scan("QQ:1:66", "B3:0:65", "B3:32:97", add, sub, 256.0)
    tt("pv", "eh", "eg", add)
    tr("QQ:66:98", "QQ:33:65")
    inc(V.tensor_scalar(T.SbT[:], T.B3[:, 0:32], T.QQ[:, 65:66], None, add), "v")
    last["SbT"] = ("v", tot["v"])
    tt("val", "QQ:64:72@repa", "CT", sub)
    tr("Sb", "SbT", sem="sb")
    scan("PP", "val", "M", O.max, mul)
    scan("P6", "val", "M6", O.max, mul)
    ts("Pu", "PP:7:64:8", 257.0 / 43, -lift, mul, add, sem="p_ok")
    tt("e1", "P6:7:64:8", "PP:7:64:8", sub)
    ts("lc", "k8", "pv", 17.0, add, O.min)
    ts("off1", "e1", -257.0, 16 + 257 * LIFT - 43 * lift, mul, add)
    need("x_in")
    quantise("x", 0)
    cp("win1:0:304@off1:0:8", "cval")
    need(*filled)
    cp("keywin:0:1536@tou:0:8", "Pf")
    tr("TR:0:288", "win1:0:288")
    tr("TR:288:576", "win1:16:304")
    quantise("x", 1)
    tt("Y1", "TR:0:576:32", "TR:16:576:32", add)
    tr("trk:0:224", "keywin:0:224")
    cp("l1", "Y1@lc", sem="l1r")
    tr("trk:224:448", "keywin:224:448")
    need("qxr")
    need("l1r")
    pickc("land1", 0, HEAD, "qx", 256, "l1", 0, 17, "q1c")
    tr("trk:448:1536", "keywin:448:1536")

    need("rc", sizes)
    tt("G", "cnt@pg", "KP", add)
    tt("Xin:64:112", "trk:0:1536:32", "trk:16:1536:32", O.max, sem="xsr")
    scan("bf", "G:0:48", "G:8:56", add, sub, 298 - 5.5)
    tt("DN", "G:0:48", "G:9:57", sub)
    for a in range(3):
        ts("NG%d" % a, "bf", 1.0 / 6, "cq:%d:%d" % (a, a + 1), mul, O.is_gt)
    for a in range(3):
        scan("S%d" % a, "DN", "NG%d" % a, add, mul)
    for a in range(3):
        ts("l2:%d:18:3" % a, "S%d:6:48:8" % a, 1.0 / 6, "cq:%d:%d" % (a, a + 1), mul, add, sem="l2r")
    ts("t3", "eh", "t2:0:1", "t2:1:2", mul, add)
    need("l2r")
    need("q1c")
    need("gd", 32)
    need("rc1", arrivals)

    for a, b in runs:
        pickc("land2", mine + 16 * a, mine + 16 * b, "land1", W1 + 1, "l2", a, b, "q2c")
    scan("MX", "DX", "XR", add, O.max)
    scan("MU", "DR", "XR", add, O.max)
    need(*made.pop("Db"))
    ts("Db:0:32:4", "MX:7:64:8", 1.0 / 6, LIFT - 2.5 / 6, mul, add)
    cp("Db:1:32:4", "MX:7:64:8")
    ts("Db:2:32:4", "MU:7:64:8", 1.0 / 6, LIFT - 2.5 / 6, mul, add)
    ts("lc2:0:1", "F4:5:6", 4.0, "t3", mul, add)
    scan("Y3:0:32", "hv", "Db", mul, add)
    need("w_in")
    quantise("w", 0)
    tr("val:16:48", "Y3:0:32")
    tr("Y3:32:96", "val")
    ts("l3", "Y3:0:96@lc2:0:1", (6.0 * OUT - 1) * LIFT, None, add, sem="l3r")
    need("l3r")
    need("q2c")
    need("rc2", arrivals)
    for h in range(2):
        pickc("q3", 128 * h, 128 * h + 128, "land2", W2, "l3", 8 * h, 8 * h + 8, "q3c%d" % h)
        if h == 0:
            quantise("w", 1)

    def part(o, h):
        return slice(256 * o + 128 * h, 256 * o + 128 * h + 128), slice(512 * (2 * o + h), 512 * (2 * o + h) + 128)

    for o, h in ((0, 0), (1, 0), (0, 1)):
        y, p = part(o, h)
        need("mm%d%d" % (o, h), 1)
        inc(V.tensor_copy(T.ys[:, y], T.ps[:, p]), "y%d%d" % (o, h))

    for h in range(2):
        w(E, "q3c%d" % h, 1)
        w(E, "q3s%d" % h, 1)
        for o in ((0, 1), (1, 0))[h]:
            if h == 0:
                w(E, "qwr", o + 1)
            inc(E.matmul_mx(T.ps[:, part(o, h)[1]], T.qw[:, 128 * o:128 * o + 128], T.sw[:, 128 * o:128 * o + 128],
                            T.q3[:, 128 * h:128 * h + 128], T.s3[:, 128 * h:128 * h + 128], True, True), "mm%d%d" % (o, h))
    y, p = part(1, 1)
    w(A, "mm11", 1)
    inc(A.activation(T.ys[:, y], T.ps[:, p], AF.Copy), "y11")
    for q, o, h in ((S, 0, 0), (S, 1, 0), (S, 0, 1), (A, 1, 1)):
        w(q, "y%d%d" % (o, h), 1)
        inc(q.dma_start(T.y[:, part(o, h)[0]], T.ys[:, part(o, h)[0]]), "st", 16)
    for s in ("v", "gi", "ac", "ls", "st"):
        w(g, s, tot[s])
